import numpy as np
import ml_dtypes


def mxq(x, axis, fmt="e4m3"):
    dtype, down = {"e4m3": (ml_dtypes.float8_e4m3fn, 7), "e5m2": (ml_dtypes.float8_e5m2, 14)}[fmt]
    v = np.moveaxis(np.asarray(x, np.float32).astype(ml_dtypes.bfloat16).astype(np.float64), axis, -1)
    blocks = v.reshape(v.shape[:-1] + (-1, 32))
    amax = np.abs(blocks).max(-1, keepdims=True)
    byte = np.maximum(np.where(amax > 0, np.frexp(amax)[1] - 1 + 127, 0) - down, 1)
    scale = np.exp2(byte - 127.0)
    codes = (blocks / scale).astype(np.float32).astype(dtype).astype(np.float64)
    return np.moveaxis((codes * scale).reshape(v.shape), -1, axis)


WIDE = False


def mx_kscale(k):
    if not WIDE:
        return np.ones(k)
    levels = np.array([10, -10, 5, -5, 0])
    if k % 512:
        return np.exp2(np.random.permutation(np.resize(levels, k // 32))).repeat(32)
    a = np.empty((k // 512, 16))
    for p in range(k // 512):
        a[p, :8] = np.random.permutation(np.resize(levels, 8))
        for g in range(8):
            far = levels[np.abs(levels - a[p, g]) >= 10]
            a[p, g + 8] = far[np.random.randint(len(far))]
    return np.exp2(a.ravel()).repeat(32)


def f64(x):
    return np.asarray(x).astype(np.float64)


def striped(idx):
    return np.tile(idx.reshape(-1, 16).T, (8, 1)).astype(np.uint16)


def unstriped(offs):
    return offs[:16].T.reshape(-1).astype(np.int64)


E2M1 = np.array([0.0, 0.5, 1.0, 1.5, 2.0, 3.0, 4.0, 6.0, -0.0, -0.5, -1.0, -1.5, -2.0, -3.0, -4.0, -6.0])


def pack_fp4(w):
    k, n = w.shape
    w = f64(np.asarray(w, np.float32).astype(ml_dtypes.bfloat16)).reshape(k // 32, 32, n)
    amax = np.abs(w).max(1)
    mant, ex = np.frexp(amax / 6.0)
    byte = np.clip(np.where(amax > 0, np.where(mant > 0.5, ex, ex - 1) + 127, 1), 1, 254)
    scaled = (w * np.exp2(127.0 - byte)[:, None, :]).reshape(k, n).astype(np.float32)
    c = np.ascontiguousarray(scaled.reshape(k // 512, 128, 4, n).transpose(0, 1, 3, 2)).astype(ml_dtypes.float4_e2m1fn).view(np.uint8) & 0xF
    words = (c[..., 0::2] | (c[..., 1::2] << 4)).reshape(k // 512, 128, 2 * n)
    return np.ascontiguousarray(words), np.ascontiguousarray(byte.astype(np.uint8).reshape(k // 512, 16, n))


def unpack_fp4(words, scales):
    g, _, n = scales.shape
    words = np.ascontiguousarray(words).reshape(g, 128, n, 2)
    nib = np.empty((g, 128, n, 4), np.uint8)
    nib[..., 0::2] = words & 0xF
    nib[..., 1::2] = words >> 4
    vals = E2M1[nib] * np.repeat(np.exp2(scales.astype(np.float64) - 127.0), 8, axis=1)[..., None]
    return vals.transpose(0, 1, 3, 2).reshape(g * 512, n)


def relu(v):
    return np.maximum(v, 0.0)


K, T, S, V, N = 512, 4096, 1024, 512, 256


def setup_inputs():
    n = np.random.standard_normal
    s = mx_kscale(K)[:, None]
    packed_w1 = pack_fp4(n((K, N)) / np.sqrt(K) / s)
    packed_w2 = pack_fp4(n((K, N)) / np.sqrt(K) / s)
    return {
        "xT": (n((K, T)) * s).astype(np.float32),
        "sT": (n((K, V)) * s).astype(np.float32),
        "w1_words": packed_w1[0],
        "w1_scales": packed_w1[1],
        "w2_words": packed_w2[0],
        "w2_scales": packed_w2[1],
        "offs": striped(np.random.permutation(T)[:S]),
        "par": striped(np.random.randint(0, V, S)),
    }


def reference(xT, sT, w1_words, w1_scales, w2_words, w2_scales, offs, par):
    xq = mxq(f64(xT)[:, unstriped(offs)], 0, "e4m3")
    y = unpack_fp4(w1_words, w1_scales).T @ xq
    t = unpack_fp4(w2_words, w2_scales).T @ mxq(f64(sT), 0, "e4m3")
    return relu(y + t[:, unstriped(par)])

@@ -1,0 +1,148 @@
+from contextlib import ExitStack
+
+import concourse.mybir as mybir
+
+K, T, S, V, N = 512, 4096, 1024, 512, 256
+FLOPS = 2 * K * N * (S + V)
+
+F32 = mybir.dt.float32
+BF16 = mybir.dt.bfloat16
+I32 = mybir.dt.int32
+U32 = mybir.dt.uint32
+U16 = mybir.dt.uint16
+U8 = mybir.dt.uint8
+FP8X4 = mybir.dt.float8_e4m3fn_x4
+FP4X4 = mybir.dt.float4_e2m1fn_x4
+ACT = mybir.ActivationFunctionType
+ALU = mybir.AluOpType
+
+P = 128
+PACK = 4
+HALF = S // 2
+LIST_COLS = 16
+PARENT_PIECE = 256
+LAST_PIECES = (1024, 1024, 1024, 512, 512)
+VECTOR_CAST_PIECE = 2
+
+
+def tile_picked_fpn_relu_e_kernel(tc, xT, sT, w1_words, w1_scales, w2_words, w2_scales, offs, par, out):
+    nc = tc.nc
+    with ExitStack() as ctx:
+        keep = ctx.enter_context(tc.tile_pool(name="keep", bufs=1))
+        psum = ctx.enter_context(tc.psum_pool(name="psum", bufs=1))
+
+        def entries(lst, start, count):
+            return lst[:, start // LIST_COLS : (start + count) // LIST_COLS]
+
+        def load_weights(queue, words, scales, name):
+            word_tile = keep.tile([P, 2 * N], U8, name=name + "_words", align_bytes=64)
+            scale_tile = keep.tile([P, N], U8, name=name + "_scales", align_bytes=64)
+            queue.dma_start(out=word_tile[:].bitcast(I32), in_=words[0].bitcast(I32))
+            for q in range(4):
+                queue.dma_start(
+                    out=scale_tile[32 * q : 32 * q + 4, :].bitcast(I32),
+                    in_=scales[0, 4 * q : 4 * q + 4, :].bitcast(I32),
+                )
+            return word_tile, scale_tile
+
+        def quantise(grouped, width, name):
+            codes = keep.tile([P, width], U32, name=name + "_codes", align_bytes=64)
+            scales = keep.tile([P, width], U8, name=name + "_scales", align_bytes=64)
+            nc.vector.quantize_mx(out=codes[:].bitcast(FP8X4), scales=scales[:], in_=grouped[:].rearrange("p w j -> p (w j)"))
+            return codes, scales
+
+        def project(weights, m, operand, name):
+            word_tile, scale_tile = weights
+            codes, scales = operand
+            acc = psum.tile([P, 512], F32, name=name)
+            nc.tensor.matmul_mx(
+                out=acc[:],
+                lhsT=word_tile[:, 2 * P * m : 2 * P * (m + 1)].bitcast(FP4X4),
+                lhsT_scale=scale_tile[:, P * m : P * (m + 1)],
+                rhs=codes[:].bitcast(FP8X4),
+                rhs_scale=scales[:],
+                start=True,
+                stop=True,
+            )
+            return acc
+
+        x_rows = xT.rearrange("(p j) t -> p j t", j=PACK)
+        planes = [keep.tile([P, T], F32, name=f"plane{j}") for j in range(PACK)]
+
+        coarse = keep.tile([P, PACK, V], F32, name="coarse")
+        nc.sync.dma_start(out=coarse[:], in_=sT.rearrange("(p j) v -> p j v", j=PACK))
+        par_list = keep.tile([P, S // LIST_COLS], U16, name="par_list")
+        nc.sync.dma_start(par_list[:], par)
+        offs_list = keep.tile([P, S // LIST_COLS], U16, name="offs_list")
+        nc.sync.dma_start(offs_list[:], offs)
+        nc.sync.dma_start(out=planes[2][:], in_=x_rows[:, 2, :])
+        w2 = load_weights(nc.scalar, w2_words, w2_scales, "w2")
+        w1 = load_weights(nc.scalar, w1_words, w1_scales, "w1")
+        for j in (0, 1):
+            nc.sync.dma_start(out=planes[j][:], in_=x_rows[:, j, :])
+        pieces = []
+        start = 0
+        for width in LAST_PIECES:
+            pieces.append(slice(start, start + width))
+            start = start + width
+        for cols in pieces:
+            nc.sync.dma_start(out=planes[3][:, cols], in_=x_rows[:, 3, cols])
+
+        coarse_grouped = keep.tile([P, V, PACK], BF16, name="coarse_grouped", align_bytes=64)
+        nc.vector.tensor_copy(
+            out=coarse_grouped[:],
+            in_=coarse[:].rearrange("p j v -> p v j"),
+        )
+        coarse_q = quantise(coarse_grouped, V, "coarse")
+        t_rows = []
+        for m in range(N // P):
+            acc = project(w2, m, coarse_q, f"t_acc{m}")
+            t_row = keep.tile([P, V], F32, name=f"t_row{m}")
+            if m == 0:
+                nc.vector.tensor_copy(out=t_row[:], in_=acc[:])
+            else:
+                nc.scalar.copy(out=t_row[:], in_=acc[:])
+            t_rows.append(t_row)
+        parents = []
+        for m in range(N // P):
+            parent = keep.tile([P, S], F32, name=f"parent{m}")
+            for s0 in range(0, S, PARENT_PIECE):
+                nc.vector.tensor_copy(
+                    out=parent[:, s0 : s0 + PARENT_PIECE],
+                    in_=t_rows[m][:].indirect(entries(par_list, s0, PARENT_PIECE)),
+                )
+            parents.append(parent)
+
+        picked = [keep.tile([P, HALF, PACK], BF16, name=f"picked{h}", align_bytes=64) for h in range(2)]
+        rounded = {j: keep.tile([P, T], BF16, name=f"rounded{j}") for j in (2, 3)}
+
+        def pick_vector(j, h):
+            nc.vector.tensor_copy(out=picked[h][:, :, j], in_=planes[j][:].indirect(entries(offs_list, h * HALF, HALF)))
+
+        def pick_scalar(j, h):
+            nc.scalar.activation(out=picked[h][:, :, j], in_=rounded[j][:].indirect(entries(offs_list, h * HALF, HALF)), func=ACT.Copy)
+
+        pick_vector(2, 0)
+        nc.scalar.copy(out=rounded[2][:], in_=planes[2][:])
+        pick_scalar(2, 1)
+        for j in (0, 1):
+            for h in range(2):
+                pick_vector(j, h)
+        for i, cols in enumerate(pieces):
+            if i == VECTOR_CAST_PIECE:
+                nc.vector.tensor_copy(out=rounded[3][:, cols], in_=planes[3][:, cols])
+            else:
+                nc.scalar.copy(out=rounded[3][:, cols], in_=planes[3][:, cols])
+        pick_vector(3, 0)
+        pick_scalar(3, 1)
+
+        fine_q = [quantise(picked[h], HALF, f"fine{h}") for h in range(2)]
+        for h in range(2):
+            for m in range(N // P):
+                acc = project(w1, m, fine_q[h], f"y_acc{h}{m}")
+                cols = slice(h * HALF, (h + 1) * HALF)
+                total = keep.tile([P, HALF], F32, name=f"total{h}{m}")
+                nc.vector.tensor_tensor(out=total[:], in0=acc[:], in1=parents[m][:, cols], op=ALU.add)
+                result = keep.tile([P, HALF], F32, name=f"result{h}{m}")
+                nc.scalar.activation(out=result[:], in_=total[:], func=ACT.Relu)
+                nc.sync.dma_start(out=out[m * P : (m + 1) * P, cols], in_=result[:])

@@ -21,8 +21,9 @@ PACK = 4
 HALF = S // 2
 LIST_COLS = 16
 PARENT_PIECE = 256
-LAST_PIECES = (1024, 1024, 1024, 512, 512)
-VECTOR_CAST_PIECE = 2
+LAST_PIECES = (1024, 1024, 1024, 512, 256, 256)
+VECTOR_CAST_PIECES = (2, 3)
+QUARTER = 256
 
 
 def tile_picked_fpn_relu_e_kernel(tc, xT, sT, w1_words, w1_scales, w2_words, w2_scales, offs, par, out):
@@ -48,15 +49,14 @@ def tile_picked_fpn_relu_e_kernel(tc, xT, sT, w1_words, w1_scales, w2_words, w2_
         def quantise(grouped, width, name):
             codes = keep.tile([P, width], U32, name=name + "_codes", align_bytes=64)
             scales = keep.tile([P, width], U8, name=name + "_scales", align_bytes=64)
-            nc.vector.quantize_mx(out=codes[:].bitcast(FP8X4), scales=scales[:], in_=grouped[:].rearrange("p w j -> p (w j)"))
+            nc.vector.quantize_mx(out=codes[:].bitcast(FP8X4), scales=scales[:], in_=grouped.rearrange("p w j -> p (w j)"))
             return codes, scales
 
-        def project(weights, m, operand, name):
+        def project(weights, m, operand, acc):
             word_tile, scale_tile = weights
             codes, scales = operand
-            acc = psum.tile([P, 512], F32, name=name)
             nc.tensor.matmul_mx(
-                out=acc[:],
+                out=acc,
                 lhsT=word_tile[:, 2 * P * m : 2 * P * (m + 1)].bitcast(FP4X4),
                 lhsT_scale=scale_tile[:, P * m : P * (m + 1)],
                 rhs=codes[:].bitcast(FP8X4),
@@ -64,7 +64,6 @@ def tile_picked_fpn_relu_e_kernel(tc, xT, sT, w1_words, w1_scales, w2_words, w2_
                 start=True,
                 stop=True,
             )
-            return acc
 
         x_rows = xT.rearrange("(p j) t -> p j t", j=PACK)
         planes = [keep.tile([P, T], F32, name=f"plane{j}") for j in range(PACK)]
@@ -74,12 +73,12 @@ def tile_picked_fpn_relu_e_kernel(tc, xT, sT, w1_words, w1_scales, w2_words, w2_
         par_list = keep.tile([P, S // LIST_COLS], U16, name="par_list")
         nc.sync.dma_start(par_list[:], par)
         offs_list = keep.tile([P, S // LIST_COLS], U16, name="offs_list")
-        nc.sync.dma_start(offs_list[:], offs)
+        w2 = load_weights(nc.sync, w2_words, w2_scales, "w2")
         nc.sync.dma_start(out=planes[2][:], in_=x_rows[:, 2, :])
-        w2 = load_weights(nc.scalar, w2_words, w2_scales, "w2")
-        w1 = load_weights(nc.scalar, w1_words, w1_scales, "w1")
-        for j in (0, 1):
-            nc.sync.dma_start(out=planes[j][:], in_=x_rows[:, j, :])
+        nc.sync.dma_start(offs_list[:], offs)
+        nc.sync.dma_start(out=planes[0][:], in_=x_rows[:, 0, :])
+        w1 = load_weights(nc.sync, w1_words, w1_scales, "w1")
+        nc.sync.dma_start(out=planes[1][:], in_=x_rows[:, 1, :])
         pieces = []
         start = 0
         for width in LAST_PIECES:
@@ -93,25 +92,24 @@ def tile_picked_fpn_relu_e_kernel(tc, xT, sT, w1_words, w1_scales, w2_words, w2_
             out=coarse_grouped[:],
             in_=coarse[:].rearrange("p j v -> p v j"),
         )
-        coarse_q = quantise(coarse_grouped, V, "coarse")
+        coarse_q = quantise(coarse_grouped[:], V, "coarse")
         t_rows = []
         for m in range(N // P):
-            acc = project(w2, m, coarse_q, f"t_acc{m}")
+            acc = psum.tile([P, V], F32, name=f"t_acc{m}")
+            project(w2, m, coarse_q, acc[:])
             t_row = keep.tile([P, V], F32, name=f"t_row{m}")
             if m == 0:
                 nc.vector.tensor_copy(out=t_row[:], in_=acc[:])
             else:
                 nc.scalar.copy(out=t_row[:], in_=acc[:])
             t_rows.append(t_row)
-        parents = []
+        parents = [keep.tile([P, N // P, QUARTER], F32, name=f"parent{c}") for c in range(S // QUARTER)]
         for m in range(N // P):
-            parent = keep.tile([P, S], F32, name=f"parent{m}")
-            for s0 in range(0, S, PARENT_PIECE):
+            for c in range(S // QUARTER):
                 nc.vector.tensor_copy(
-                    out=parent[:, s0 : s0 + PARENT_PIECE],
-                    in_=t_rows[m][:].indirect(entries(par_list, s0, PARENT_PIECE)),
+                    out=parents[c][:, m, :],
+                    in_=t_rows[m][:].indirect(entries(par_list, c * QUARTER, QUARTER)),
                 )
-            parents.append(parent)
 
         picked = [keep.tile([P, HALF, PACK], BF16, name=f"picked{h}", align_bytes=64) for h in range(2)]
         rounded = {j: keep.tile([P, T], BF16, name=f"rounded{j}") for j in (2, 3)}
@@ -129,20 +127,40 @@ def tile_picked_fpn_relu_e_kernel(tc, xT, sT, w1_words, w1_scales, w2_words, w2_
             for h in range(2):
                 pick_vector(j, h)
         for i, cols in enumerate(pieces):
-            if i == VECTOR_CAST_PIECE:
+            if i in VECTOR_CAST_PIECES:
                 nc.vector.tensor_copy(out=rounded[3][:, cols], in_=planes[3][:, cols])
             else:
                 nc.scalar.copy(out=rounded[3][:, cols], in_=planes[3][:, cols])
         pick_vector(3, 0)
         pick_scalar(3, 1)
 
-        fine_q = [quantise(picked[h], HALF, f"fine{h}") for h in range(2)]
-        for h in range(2):
+        out_rows = out.rearrange("(m p) s -> p m s", p=P)
+        last = S // QUARTER - 1
+        sums = []
+
+        def multiply(c):
+            h, first = divmod(c * QUARTER, HALF)
+            fine_q = quantise(picked[h][:, first : first + QUARTER, :], QUARTER, f"fine{c}")
+            acc = psum.tile([P, N // P, QUARTER], F32, name=f"y_acc{c}")
             for m in range(N // P):
-                acc = project(w1, m, fine_q[h], f"y_acc{h}{m}")
-                cols = slice(h * HALF, (h + 1) * HALF)
-                total = keep.tile([P, HALF], F32, name=f"total{h}{m}")
-                nc.vector.tensor_tensor(out=total[:], in0=acc[:], in1=parents[m][:, cols], op=ALU.add)
-                result = keep.tile([P, HALF], F32, name=f"result{h}{m}")
+                project(w1, m, fine_q, acc[:, m, :])
+            sums.append(acc)
+
+        def finish(c):
+            cols = slice(c * QUARTER, (c + 1) * QUARTER)
+            spans = [slice(0, 1), slice(1, 2)] if c == last else [slice(0, 2)]
+            for i, ms in enumerate(spans):
+                width = ms.stop - ms.start
+                total = keep.tile([P, width, QUARTER], F32, name=f"total{c}_{i}")
+                nc.vector.tensor_tensor(out=total[:], in0=sums[c][:, ms, :], in1=parents[c][:, ms, :], op=ALU.add)
+                result = keep.tile([P, width, QUARTER], F32, name=f"result{c}_{i}")
                 nc.scalar.activation(out=result[:], in_=total[:], func=ACT.Relu)
-                nc.sync.dma_start(out=out[m * P : (m + 1) * P, cols], in_=result[:])
+                nc.sync.dma_start(out=out_rows[:, ms, cols], in_=result[:])
+
+        multiply(0)
+        multiply(1)
+        finish(0)
+        multiply(2)
+        multiply(3)
+        for c in range(1, S // QUARTER):
+            finish(c)

@@ -24,6 +24,7 @@ PARENT_PIECE = 256
 LAST_PIECES = (1024, 1024, 1024, 512, 256, 256)
 VECTOR_CAST_PIECES = (2, 3)
 QUARTER = 256
+WEAVE_SPLIT = 336
 
 
 def tile_picked_fpn_relu_e_kernel(tc, xT, sT, w1_words, w1_scales, w2_words, w2_scales, offs, par, out):
@@ -89,8 +90,12 @@ def tile_picked_fpn_relu_e_kernel(tc, xT, sT, w1_words, w1_scales, w2_words, w2_
 
         coarse_grouped = keep.tile([P, V, PACK], BF16, name="coarse_grouped", align_bytes=64)
         nc.vector.tensor_copy(
-            out=coarse_grouped[:],
-            in_=coarse[:].rearrange("p j v -> p v j"),
+            out=coarse_grouped[:, :WEAVE_SPLIT, :].rearrange("p (c i) j -> p c j i", i=4),
+            in_=coarse[:, :, :WEAVE_SPLIT].rearrange("p j (c i) -> p c j i", i=4),
+        )
+        nc.scalar.copy(
+            out=coarse_grouped[:, WEAVE_SPLIT:, :].rearrange("p (c i) j -> p c j i", i=4),
+            in_=coarse[:, :, WEAVE_SPLIT:].rearrange("p j (c i) -> p c j i", i=4),
         )
         coarse_q = quantise(coarse_grouped[:], V, "coarse")
         t_rows = []
@@ -112,7 +117,7 @@ def tile_picked_fpn_relu_e_kernel(tc, xT, sT, w1_words, w1_scales, w2_words, w2_
                 )
 
         picked = [keep.tile([P, HALF, PACK], BF16, name=f"picked{h}", align_bytes=64) for h in range(2)]
-        rounded = {j: keep.tile([P, T], BF16, name=f"rounded{j}") for j in (2, 3)}
+        rounded = {2: keep.tile([P, T], BF16, name="rounded2", tag="rounded")}
 
         def pick_vector(j, h):
             nc.vector.tensor_copy(out=picked[h][:, :, j], in_=planes[j][:].indirect(entries(offs_list, h * HALF, HALF)))
@@ -120,12 +125,13 @@ def tile_picked_fpn_relu_e_kernel(tc, xT, sT, w1_words, w1_scales, w2_words, w2_
         def pick_scalar(j, h):
             nc.scalar.activation(out=picked[h][:, :, j], in_=rounded[j][:].indirect(entries(offs_list, h * HALF, HALF)), func=ACT.Copy)
 
-        pick_vector(2, 0)
         nc.scalar.copy(out=rounded[2][:], in_=planes[2][:])
+        pick_scalar(2, 0)
         pick_scalar(2, 1)
         for j in (0, 1):
             for h in range(2):
                 pick_vector(j, h)
+        rounded[3] = keep.tile([P, T], BF16, name="rounded3", tag="rounded")
         for i, cols in enumerate(pieces):
             if i in VECTOR_CAST_PIECES:
                 nc.vector.tensor_copy(out=rounded[3][:, cols], in_=planes[3][:, cols])
@@ -148,7 +154,7 @@ def tile_picked_fpn_relu_e_kernel(tc, xT, sT, w1_words, w1_scales, w2_words, w2_
 
         def finish(c):
             cols = slice(c * QUARTER, (c + 1) * QUARTER)
-            spans = [slice(0, 1), slice(1, 2)] if c == last else [slice(0, 2)]
+            spans = [slice(0, 1), slice(1, 2)] if c in (0, last) else [slice(0, 2)]
             for i, ms in enumerate(spans):
                 width = ms.stop - ms.start
                 total = keep.tile([P, width, QUARTER], F32, name=f"total{c}_{i}")

@@ -21,8 +21,8 @@ PACK = 4
 HALF = S // 2
 LIST_COLS = 16
 PARENT_PIECE = 256
-LAST_PIECES = (1024, 1024, 1024, 512, 256, 256)
-VECTOR_CAST_PIECES = (2, 3)
+LAST_PIECES = (1024, 1024, 1024, 512, 512)
+VECTOR_CAST_PIECES = (2,)
 QUARTER = 256
 WEAVE_SPLIT = 336
 
@@ -47,8 +47,8 @@ def tile_picked_fpn_relu_e_kernel(tc, xT, sT, w1_words, w1_scales, w2_words, w2_
                 )
             return word_tile, scale_tile
 
-        def quantise(grouped, width, name):
-            codes = keep.tile([P, width], U32, name=name + "_codes", align_bytes=64)
+        def quantise(grouped, width, name, tag):
+            codes = keep.tile([P, width], U32, name=name + "_codes", tag=tag, align_bytes=64)
             scales = keep.tile([P, width], U8, name=name + "_scales", align_bytes=64)
             nc.vector.quantize_mx(out=codes[:].bitcast(FP8X4), scales=scales[:], in_=grouped.rearrange("p w j -> p (w j)"))
             return codes, scales
@@ -78,7 +78,6 @@ def tile_picked_fpn_relu_e_kernel(tc, xT, sT, w1_words, w1_scales, w2_words, w2_
         nc.sync.dma_start(out=planes[2][:], in_=x_rows[:, 2, :])
         nc.sync.dma_start(offs_list[:], offs)
         nc.sync.dma_start(out=planes[0][:], in_=x_rows[:, 0, :])
-        w1 = load_weights(nc.sync, w1_words, w1_scales, "w1")
         nc.sync.dma_start(out=planes[1][:], in_=x_rows[:, 1, :])
         pieces = []
         start = 0
@@ -87,6 +86,7 @@ def tile_picked_fpn_relu_e_kernel(tc, xT, sT, w1_words, w1_scales, w2_words, w2_
             start = start + width
         for cols in pieces:
             nc.sync.dma_start(out=planes[3][:, cols], in_=x_rows[:, 3, cols])
+        w1 = load_weights(nc.sync, w1_words, w1_scales, "w1")
 
         coarse_grouped = keep.tile([P, V, PACK], BF16, name="coarse_grouped", align_bytes=64)
         nc.vector.tensor_copy(
@@ -97,7 +97,7 @@ def tile_picked_fpn_relu_e_kernel(tc, xT, sT, w1_words, w1_scales, w2_words, w2_
             out=coarse_grouped[:, WEAVE_SPLIT:, :].rearrange("p (c i) j -> p c j i", i=4),
             in_=coarse[:, :, WEAVE_SPLIT:].rearrange("p j (c i) -> p c j i", i=4),
         )
-        coarse_q = quantise(coarse_grouped[:], V, "coarse")
+        coarse_q = quantise(coarse_grouped[:], V, "coarse", "coarse_codes")
         t_rows = []
         for m in range(N // P):
             acc = psum.tile([P, V], F32, name=f"t_acc{m}")
@@ -108,11 +108,16 @@ def tile_picked_fpn_relu_e_kernel(tc, xT, sT, w1_words, w1_scales, w2_words, w2_
             else:
                 nc.scalar.copy(out=t_row[:], in_=acc[:])
             t_rows.append(t_row)
-        parents = [keep.tile([P, N // P, QUARTER], F32, name=f"parent{c}") for c in range(S // QUARTER)]
+        first_parents = [keep.tile([P, 1, QUARTER], F32, name=f"first_parent{m}", tag=f"shared{m}", align_bytes=64) for m in range(N // P)]
+        parents = [None] + [keep.tile([P, N // P, QUARTER], F32, name=f"parent{c}") for c in range(1, S // QUARTER)]
+
+        def parent_of(c, ms):
+            return first_parents[ms.start][:] if c == 0 else parents[c][:, ms, :]
+
         for m in range(N // P):
             for c in range(S // QUARTER):
                 nc.vector.tensor_copy(
-                    out=parents[c][:, m, :],
+                    out=parent_of(c, slice(m, m + 1))[:, 0, :],
                     in_=t_rows[m][:].indirect(entries(par_list, c * QUARTER, QUARTER)),
                 )
 
@@ -146,7 +151,7 @@ def tile_picked_fpn_relu_e_kernel(tc, xT, sT, w1_words, w1_scales, w2_words, w2_
 
         def multiply(c):
             h, first = divmod(c * QUARTER, HALF)
-            fine_q = quantise(picked[h][:, first : first + QUARTER, :], QUARTER, f"fine{c}")
+            fine_q = quantise(picked[h][:, first : first + QUARTER, :], QUARTER, f"fine{c}", "shared1" if c == last else f"fine{c}_codes")
             acc = psum.tile([P, N // P, QUARTER], F32, name=f"y_acc{c}")
             for m in range(N // P):
                 project(w1, m, fine_q, acc[:, m, :])
@@ -158,15 +163,16 @@ def tile_picked_fpn_relu_e_kernel(tc, xT, sT, w1_words, w1_scales, w2_words, w2_
             for i, ms in enumerate(spans):
                 width = ms.stop - ms.start
                 total = keep.tile([P, width, QUARTER], F32, name=f"total{c}_{i}")
-                nc.vector.tensor_tensor(out=total[:], in0=sums[c][:, ms, :], in1=parents[c][:, ms, :], op=ALU.add)
+                nc.vector.tensor_tensor(out=total[:], in0=sums[c][:, ms, :], in1=parent_of(c, ms), op=ALU.add)
                 result = keep.tile([P, width, QUARTER], F32, name=f"result{c}_{i}")
                 nc.scalar.activation(out=result[:], in_=total[:], func=ACT.Relu)
-                nc.sync.dma_start(out=out_rows[:, ms, cols], in_=result[:])
+                queue = nc.scalar if c == last and ms.stop == N // P else nc.sync
+                queue.dma_start(out=out_rows[:, ms, cols], in_=result[:])
 
         multiply(0)
         multiply(1)
-        finish(0)
         multiply(2)
+        finish(0)
         multiply(3)
         for c in range(1, S // QUARTER):
             finish(c)

@@ -20,7 +20,6 @@ P = 128
 PACK = 4
 HALF = S // 2
 LIST_COLS = 16
-PARENT_PIECE = 256
 LAST_PIECES = (1024, 1024, 1024, 512, 512)
 VECTOR_CAST_PIECES = (2,)
 QUARTER = 256
@@ -100,7 +99,7 @@ def tile_picked_fpn_relu_e_kernel(tc, xT, sT, w1_words, w1_scales, w2_words, w2_
         coarse_q = quantise(coarse_grouped[:], V, "coarse", "coarse_codes")
         t_rows = []
         for m in range(N // P):
-            acc = psum.tile([P, V], F32, name=f"t_acc{m}")
+            acc = psum.tile([P, V], F32, name=f"t_acc{m}", tag=f"bank{6 + m}")
             project(w2, m, coarse_q, acc[:])
             t_row = keep.tile([P, V], F32, name=f"t_row{m}")
             if m == 0:
@@ -108,16 +107,13 @@ def tile_picked_fpn_relu_e_kernel(tc, xT, sT, w1_words, w1_scales, w2_words, w2_
             else:
                 nc.scalar.copy(out=t_row[:], in_=acc[:])
             t_rows.append(t_row)
-        first_parents = [keep.tile([P, 1, QUARTER], F32, name=f"first_parent{m}", tag=f"shared{m}", align_bytes=64) for m in range(N // P)]
-        parents = [None] + [keep.tile([P, N // P, QUARTER], F32, name=f"parent{c}") for c in range(1, S // QUARTER)]
-
-        def parent_of(c, ms):
-            return first_parents[ms.start][:] if c == 0 else parents[c][:, ms, :]
-
+        quarters = S // QUARTER
+        parents = {}
         for m in range(N // P):
-            for c in range(S // QUARTER):
+            for c in range(quarters):
+                parents[c, m] = keep.tile([P, QUARTER], F32, name=f"parent{c}_{m}", tag=f"parent{c}_{m}", align_bytes=64)
                 nc.vector.tensor_copy(
-                    out=parent_of(c, slice(m, m + 1))[:, 0, :],
+                    out=parents[c, m][:],
                     in_=t_rows[m][:].indirect(entries(par_list, c * QUARTER, QUARTER)),
                 )
 
@@ -145,34 +141,30 @@ def tile_picked_fpn_relu_e_kernel(tc, xT, sT, w1_words, w1_scales, w2_words, w2_
         pick_vector(3, 0)
         pick_scalar(3, 1)
 
-        out_rows = out.rearrange("(m p) s -> p m s", p=P)
-        last = S // QUARTER - 1
-        sums = []
+        last = quarters - 1
+        sums = {}
 
         def multiply(c):
             h, first = divmod(c * QUARTER, HALF)
-            fine_q = quantise(picked[h][:, first : first + QUARTER, :], QUARTER, f"fine{c}", "shared1" if c == last else f"fine{c}_codes")
-            acc = psum.tile([P, N // P, QUARTER], F32, name=f"y_acc{c}")
+            fine_q = quantise(picked[h][:, first : first + QUARTER, :], QUARTER, f"fine{c}", "parent0_0" if c == last else f"fine{c}_codes")
             for m in range(N // P):
-                project(w1, m, fine_q, acc[:, m, :])
-            sums.append(acc)
+                sums[c, m] = psum.tile([P, QUARTER], F32, name=f"y_acc{c}_{m}", tag=f"bank{2 * c + m}")
+                project(w1, m, fine_q, sums[c, m][:])
 
         def finish(c):
             cols = slice(c * QUARTER, (c + 1) * QUARTER)
-            spans = [slice(0, 1), slice(1, 2)] if c in (0, last) else [slice(0, 2)]
-            for i, ms in enumerate(spans):
-                width = ms.stop - ms.start
-                total = keep.tile([P, width, QUARTER], F32, name=f"total{c}_{i}")
-                nc.vector.tensor_tensor(out=total[:], in0=sums[c][:, ms, :], in1=parent_of(c, ms), op=ALU.add)
-                result = keep.tile([P, width, QUARTER], F32, name=f"result{c}_{i}")
+            for m in range(N // P):
+                total = keep.tile([P, QUARTER], F32, name=f"total{c}_{m}")
+                nc.vector.tensor_tensor(out=total[:], in0=sums[c, m][:], in1=parents[c, m][:], op=ALU.add)
+                result = keep.tile([P, QUARTER], F32, name=f"result{c}_{m}")
                 nc.scalar.activation(out=result[:], in_=total[:], func=ACT.Relu)
-                queue = nc.scalar if c == last and ms.stop == N // P else nc.sync
-                queue.dma_start(out=out_rows[:, ms, cols], in_=result[:])
+                queue = nc.scalar if c == last and m == N // P - 1 else nc.sync
+                queue.dma_start(out=out[m * P : (m + 1) * P, cols], in_=result[:])
 
         multiply(0)
         multiply(1)
         multiply(2)
         finish(0)
         multiply(3)
-        for c in range(1, S // QUARTER):
+        for c in range(1, quarters):
             finish(c)

@@ -20,9 +20,9 @@ P = 128
 PACK = 4
 HALF = S // 2
 LIST_COLS = 16
-LAST_PIECES = (1024, 1024, 1024, 512, 512)
-VECTOR_CAST_PIECES = (2,)
-QUARTER = 256
+LAST_PIECES = (1024, 1024, 1024, 512, 256, 256)
+VECTOR_CAST_PIECES = (2, 4)
+STRETCHES = (128, 128, 256, 256, 256)
 WEAVE_SPLIT = 336
 
 
@@ -107,15 +107,25 @@ def tile_picked_fpn_relu_e_kernel(tc, xT, sT, w1_words, w1_scales, w2_words, w2_
             else:
                 nc.scalar.copy(out=t_row[:], in_=acc[:])
             t_rows.append(t_row)
-        quarters = S // QUARTER
+        row_tiles = N // P
+        stretches = []
+        first = 0
+        for width in STRETCHES:
+            stretches.append((first, width))
+            first = first + width
+        items = []
+        for c in range(len(stretches)):
+            items.extend([(c, 0, row_tiles)] if c == 1 else [(c, m, 1) for m in range(row_tiles)])
         parents = {}
-        for m in range(N // P):
-            for c in range(quarters):
-                parents[c, m] = keep.tile([P, QUARTER], F32, name=f"parent{c}_{m}", tag=f"parent{c}_{m}", align_bytes=64)
-                nc.vector.tensor_copy(
-                    out=parents[c, m][:],
-                    in_=t_rows[m][:].indirect(entries(par_list, c * QUARTER, QUARTER)),
-                )
+        for c, m0, count in items:
+            parents[c, m0] = keep.tile([P, count, stretches[c][1]], F32, name=f"parent{c}_{m0}", tag=f"parent{c}_{m0}", align_bytes=64)
+        for m in range(row_tiles):
+            for c, m0, count in items:
+                if m0 <= m < m0 + count:
+                    nc.vector.tensor_copy(
+                        out=parents[c, m0][:, m - m0, :],
+                        in_=t_rows[m][:].indirect(entries(par_list, *stretches[c])),
+                    )
 
         picked = [keep.tile([P, HALF, PACK], BF16, name=f"picked{h}", align_bytes=64) for h in range(2)]
         rounded = {2: keep.tile([P, T], BF16, name="rounded2", tag="rounded")}
@@ -141,30 +151,36 @@ def tile_picked_fpn_relu_e_kernel(tc, xT, sT, w1_words, w1_scales, w2_words, w2_
         pick_vector(3, 0)
         pick_scalar(3, 1)
 
-        last = quarters - 1
+        out_rows = out.rearrange("(m p) s -> p m s", p=P)
         sums = {}
+        held = {4: "parent0_0"}
 
         def multiply(c):
-            h, first = divmod(c * QUARTER, HALF)
-            fine_q = quantise(picked[h][:, first : first + QUARTER, :], QUARTER, f"fine{c}", "parent0_0" if c == last else f"fine{c}_codes")
-            for m in range(N // P):
-                sums[c, m] = psum.tile([P, QUARTER], F32, name=f"y_acc{c}_{m}", tag=f"bank{2 * c + m}")
-                project(w1, m, fine_q, sums[c, m][:])
+            start, width = stretches[c]
+            h, first = divmod(start, HALF)
+            fine_q = quantise(picked[h][:, first : first + width, :], width, f"fine{c}", held.get(c, f"fine{c}_codes"))
+            for i, (ci, m0, count) in enumerate(items):
+                if ci == c:
+                    sums[c, m0] = psum.tile([P, count, width], F32, name=f"y_acc{c}_{m0}", tag=f"bank{i % 8}")
+                    for m in range(count):
+                        project(w1, m0 + m, fine_q, sums[c, m0][:, m, :])
 
         def finish(c):
-            cols = slice(c * QUARTER, (c + 1) * QUARTER)
-            for m in range(N // P):
-                total = keep.tile([P, QUARTER], F32, name=f"total{c}_{m}")
-                nc.vector.tensor_tensor(out=total[:], in0=sums[c, m][:], in1=parents[c, m][:], op=ALU.add)
-                result = keep.tile([P, QUARTER], F32, name=f"result{c}_{m}")
-                nc.scalar.activation(out=result[:], in_=total[:], func=ACT.Relu)
-                queue = nc.scalar if c == last and m == N // P - 1 else nc.sync
-                queue.dma_start(out=out[m * P : (m + 1) * P, cols], in_=result[:])
+            start, width = stretches[c]
+            for ci, m0, count in items:
+                if ci == c:
+                    total = keep.tile([P, count, width], F32, name=f"total{c}_{m0}")
+                    nc.vector.tensor_tensor(out=total[:], in0=sums[c, m0][:], in1=parents[c, m0][:], op=ALU.add)
+                    result = keep.tile([P, count, width], F32, name=f"result{c}_{m0}")
+                    nc.scalar.activation(out=result[:], in_=total[:], func=ACT.Relu)
+                    queue = nc.scalar if (ci, m0, count) == items[-1] else nc.sync
+                    queue.dma_start(out=out_rows[:, m0 : m0 + count, start : start + width], in_=result[:])
 
         multiply(0)
         multiply(1)
         multiply(2)
-        finish(0)
         multiply(3)
-        for c in range(1, quarters):
+        finish(0)
+        multiply(4)
+        for c in range(1, len(stretches)):
             finish(c)

@@ -20,8 +20,9 @@ P = 128
 PACK = 4
 HALF = S // 2
 LIST_COLS = 16
-LAST_PIECES = (1024, 1024, 1024, 512, 256, 256)
-VECTOR_CAST_PIECES = (2, 4)
+LAST_PIECES = (1536, 1600, 704, 256)
+VECTOR_CAST_COLUMNS = (0, 1088, 448, 0)
+VECTOR_CAST_PLANE2 = 1792
 STRETCHES = (128, 128, 256, 256, 256)
 WEAVE_SPLIT = 336
 
@@ -66,7 +67,10 @@ def tile_picked_fpn_relu_e_kernel(tc, xT, sT, w1_words, w1_scales, w2_words, w2_
             )
 
         x_rows = xT.rearrange("(p j) t -> p j t", j=PACK)
-        planes = [keep.tile([P, T], F32, name=f"plane{j}") for j in range(PACK)]
+        middle = keep.tile([P, 2, T], F32, name="planes12")
+        plane0 = keep.tile([P, T], F32, name="plane0")
+        plane3 = keep.tile([P, T], F32, name="plane3")
+        planes = [plane0[:], middle[:, 0, :], middle[:, 1, :], plane3[:]]
 
         coarse = keep.tile([P, PACK, V], F32, name="coarse")
         nc.sync.dma_start(out=coarse[:], in_=sT.rearrange("(p j) v -> p j v", j=PACK))
@@ -74,10 +78,9 @@ def tile_picked_fpn_relu_e_kernel(tc, xT, sT, w1_words, w1_scales, w2_words, w2_
         nc.sync.dma_start(par_list[:], par)
         offs_list = keep.tile([P, S // LIST_COLS], U16, name="offs_list")
         w2 = load_weights(nc.sync, w2_words, w2_scales, "w2")
-        nc.sync.dma_start(out=planes[2][:], in_=x_rows[:, 2, :])
+        nc.sync.dma_start(out=middle[:], in_=x_rows[:, 1:3, :])
         nc.sync.dma_start(offs_list[:], offs)
-        nc.sync.dma_start(out=planes[0][:], in_=x_rows[:, 0, :])
-        nc.sync.dma_start(out=planes[1][:], in_=x_rows[:, 1, :])
+        nc.sync.dma_start(out=planes[0], in_=x_rows[:, 0, :])
         pieces = []
         start = 0
         for width in LAST_PIECES:
@@ -131,23 +134,26 @@ def tile_picked_fpn_relu_e_kernel(tc, xT, sT, w1_words, w1_scales, w2_words, w2_
         rounded = {2: keep.tile([P, T], BF16, name="rounded2", tag="rounded")}
 
         def pick_vector(j, h):
-            nc.vector.tensor_copy(out=picked[h][:, :, j], in_=planes[j][:].indirect(entries(offs_list, h * HALF, HALF)))
+            nc.vector.tensor_copy(out=picked[h][:, :, j], in_=planes[j].indirect(entries(offs_list, h * HALF, HALF)))
 
         def pick_scalar(j, h):
             nc.scalar.activation(out=picked[h][:, :, j], in_=rounded[j][:].indirect(entries(offs_list, h * HALF, HALF)), func=ACT.Copy)
 
-        nc.scalar.copy(out=rounded[2][:], in_=planes[2][:])
+        def round_shared(j, cols, vector_columns):
+            middle_col = cols.start + vector_columns
+            if vector_columns > 0:
+                nc.vector.tensor_copy(out=rounded[j][:, cols.start : middle_col], in_=planes[j][:, cols.start : middle_col])
+            nc.scalar.copy(out=rounded[j][:, middle_col : cols.stop], in_=planes[j][:, middle_col : cols.stop])
+
+        round_shared(2, slice(0, T), VECTOR_CAST_PLANE2)
         pick_scalar(2, 0)
         pick_scalar(2, 1)
-        for j in (0, 1):
+        for j in (1, 0):
             for h in range(2):
                 pick_vector(j, h)
         rounded[3] = keep.tile([P, T], BF16, name="rounded3", tag="rounded")
-        for i, cols in enumerate(pieces):
-            if i in VECTOR_CAST_PIECES:
-                nc.vector.tensor_copy(out=rounded[3][:, cols], in_=planes[3][:, cols])
-            else:
-                nc.scalar.copy(out=rounded[3][:, cols], in_=planes[3][:, cols])
+        for cols, vector_columns in zip(pieces, VECTOR_CAST_COLUMNS):
+            round_shared(3, cols, vector_columns)
         pick_vector(3, 0)
         pick_scalar(3, 1)
 

@@ -23,7 +23,7 @@ LIST_COLS = 16
 LAST_PIECES = (1536, 1600, 704, 256)
 VECTOR_CAST_COLUMNS = (0, 1088, 448, 0)
 VECTOR_CAST_PLANE2 = 1792
-STRETCHES = (128, 128, 256, 256, 256)
+STRETCHES = (256, 256, 256, 256)
 WEAVE_SPLIT = 336
 
 
@@ -118,7 +118,7 @@ def tile_picked_fpn_relu_e_kernel(tc, xT, sT, w1_words, w1_scales, w2_words, w2_
             first = first + width
         items = []
         for c in range(len(stretches)):
-            items.extend([(c, 0, row_tiles)] if c == 1 else [(c, m, 1) for m in range(row_tiles)])
+            items.extend([(c, m, 1) for m in range(row_tiles)])
         parents = {}
         for c, m0, count in items:
             parents[c, m0] = keep.tile([P, count, stretches[c][1]], F32, name=f"parent{c}_{m0}", tag=f"parent{c}_{m0}", align_bytes=64)
@@ -159,12 +159,11 @@ def tile_picked_fpn_relu_e_kernel(tc, xT, sT, w1_words, w1_scales, w2_words, w2_
 
         out_rows = out.rearrange("(m p) s -> p m s", p=P)
         sums = {}
-        held = {4: "parent0_0"}
 
         def multiply(c):
             start, width = stretches[c]
             h, first = divmod(start, HALF)
-            fine_q = quantise(picked[h][:, first : first + width, :], width, f"fine{c}", held.get(c, f"fine{c}_codes"))
+            fine_q = quantise(picked[h][:, first : first + width, :], width, f"fine{c}", f"fine{c}_codes")
             for i, (ci, m0, count) in enumerate(items):
                 if ci == c:
                     sums[c, m0] = psum.tile([P, count, width], F32, name=f"y_acc{c}_{m0}", tag=f"bank{i % 8}")
@@ -182,11 +181,7 @@ def tile_picked_fpn_relu_e_kernel(tc, xT, sT, w1_words, w1_scales, w2_words, w2_
                     queue = nc.scalar if (ci, m0, count) == items[-1] else nc.sync
                     queue.dma_start(out=out_rows[:, m0 : m0 + count, start : start + width], in_=result[:])
 
-        multiply(0)
-        multiply(1)
-        multiply(2)
-        multiply(3)
-        finish(0)
-        multiply(4)
-        for c in range(1, len(stretches)):
+        for c in range(len(stretches)):
+            multiply(c)
+        for c in range(len(stretches)):
             finish(c)

@@ -18,13 +18,17 @@ ALU = mybir.AluOpType
 
 P = 128
 PACK = 4
+ROW_TILES = N // P
 HALF = S // 2
-LIST_COLS = 16
-LAST_PIECES = (1536, 1600, 704, 256)
-VECTOR_CAST_COLUMNS = (0, 1088, 448, 0)
-VECTOR_CAST_PLANE2 = 1792
-STRETCHES = (256, 256, 256, 256)
-WEAVE_SPLIT = 336
+STRETCH = 256
+LIST_ROWS = 16
+QUADRANT = 32
+RUN = 4
+
+LAST_PLANE_PIECES = ((1536, 0), (1600, 1088), (704, 448), (256, 0))
+PLANE2_VECTOR_COLUMNS = 1792
+COARSE_VECTOR_COLUMNS = 336
+PARENT_WINDOW = 1408
 
 
 def tile_picked_fpn_relu_e_kernel(tc, xT, sT, w1_words, w1_scales, w2_words, w2_scales, offs, par, out):
@@ -33,22 +37,22 @@ def tile_picked_fpn_relu_e_kernel(tc, xT, sT, w1_words, w1_scales, w2_words, w2_
         keep = ctx.enter_context(tc.tile_pool(name="keep", bufs=1))
         psum = ctx.enter_context(tc.psum_pool(name="psum", bufs=1))
 
-        def entries(lst, start, count):
-            return lst[:, start // LIST_COLS : (start + count) // LIST_COLS]
+        def entries(list_tile, start, count):
+            return list_tile[:, start // LIST_ROWS : (start + count) // LIST_ROWS]
 
-        def load_weights(queue, words, scales, name):
+        def load_weights(words, scales, name):
             word_tile = keep.tile([P, 2 * N], U8, name=name + "_words", align_bytes=64)
             scale_tile = keep.tile([P, N], U8, name=name + "_scales", align_bytes=64)
-            queue.dma_start(out=word_tile[:].bitcast(I32), in_=words[0].bitcast(I32))
-            for q in range(4):
-                queue.dma_start(
-                    out=scale_tile[32 * q : 32 * q + 4, :].bitcast(I32),
+            nc.sync.dma_start(out=word_tile[:].bitcast(I32), in_=words[0].bitcast(I32))
+            for q in range(P // QUADRANT):
+                nc.sync.dma_start(
+                    out=scale_tile[QUADRANT * q : QUADRANT * q + 4, :].bitcast(I32),
                     in_=scales[0, 4 * q : 4 * q + 4, :].bitcast(I32),
                 )
             return word_tile, scale_tile
 
-        def quantise(grouped, width, name, tag):
-            codes = keep.tile([P, width], U32, name=name + "_codes", tag=tag, align_bytes=64)
+        def quantise(grouped, width, name):
+            codes = keep.tile([P, width], U32, name=name + "_codes", align_bytes=64)
             scales = keep.tile([P, width], U8, name=name + "_scales", align_bytes=64)
             nc.vector.quantize_mx(out=codes[:].bitcast(FP8X4), scales=scales[:], in_=grouped.rearrange("p w j -> p (w j)"))
             return codes, scales
@@ -67,121 +71,85 @@ def tile_picked_fpn_relu_e_kernel(tc, xT, sT, w1_words, w1_scales, w2_words, w2_
             )
 
         x_rows = xT.rearrange("(p j) t -> p j t", j=PACK)
-        middle = keep.tile([P, 2, T], F32, name="planes12")
         plane0 = keep.tile([P, T], F32, name="plane0")
+        planes12 = keep.tile([P, 2, T], F32, name="planes12")
         plane3 = keep.tile([P, T], F32, name="plane3")
-        planes = [plane0[:], middle[:, 0, :], middle[:, 1, :], plane3[:]]
+        planes = [plane0[:], planes12[:, 0, :], planes12[:, 1, :], plane3[:]]
 
-        coarse = keep.tile([P, PACK, V], F32, name="coarse")
-        nc.sync.dma_start(out=coarse[:], in_=sT.rearrange("(p j) v -> p j v", j=PACK))
-        par_list = keep.tile([P, S // LIST_COLS], U16, name="par_list")
+        coarse_tile = keep.tile([P, (ROW_TILES + PACK) * V], F32, name="coarse_tile")
+        coarse = coarse_tile[:, ROW_TILES * V :].rearrange("p (j v) -> p j v", j=PACK)
+        nc.sync.dma_start(out=coarse, in_=sT.rearrange("(p j) v -> p j v", j=PACK))
+        par_list = keep.tile([P, S // LIST_ROWS], U16, name="par_list")
         nc.sync.dma_start(par_list[:], par)
-        offs_list = keep.tile([P, S // LIST_COLS], U16, name="offs_list")
-        w2 = load_weights(nc.sync, w2_words, w2_scales, "w2")
-        nc.sync.dma_start(out=middle[:], in_=x_rows[:, 1:3, :])
+        w2 = load_weights(w2_words, w2_scales, "w2")
+        nc.sync.dma_start(out=planes12[:], in_=x_rows[:, 1:3, :])
+        offs_list = keep.tile([P, S // LIST_ROWS], U16, name="offs_list")
         nc.sync.dma_start(offs_list[:], offs)
         nc.sync.dma_start(out=planes[0], in_=x_rows[:, 0, :])
         pieces = []
-        start = 0
-        for width in LAST_PIECES:
-            pieces.append(slice(start, start + width))
-            start = start + width
-        for cols in pieces:
-            nc.sync.dma_start(out=planes[3][:, cols], in_=x_rows[:, 3, cols])
-        w1 = load_weights(nc.sync, w1_words, w1_scales, "w1")
+        first = 0
+        for width, vector_columns in LAST_PLANE_PIECES:
+            pieces.append((first, first + vector_columns, first + width))
+            first = first + width
+        for first, split, last in pieces:
+            nc.sync.dma_start(out=planes[3][:, first:last], in_=x_rows[:, 3, first:last])
+        w1 = load_weights(w1_words, w1_scales, "w1")
 
         coarse_grouped = keep.tile([P, V, PACK], BF16, name="coarse_grouped", align_bytes=64)
         nc.vector.tensor_copy(
-            out=coarse_grouped[:, :WEAVE_SPLIT, :].rearrange("p (c i) j -> p c j i", i=4),
-            in_=coarse[:, :, :WEAVE_SPLIT].rearrange("p j (c i) -> p c j i", i=4),
+            out=coarse_grouped[:, :COARSE_VECTOR_COLUMNS, :].rearrange("p (c i) j -> p c j i", i=RUN),
+            in_=coarse[:, :, :COARSE_VECTOR_COLUMNS].rearrange("p j (c i) -> p c j i", i=RUN),
         )
         nc.scalar.copy(
-            out=coarse_grouped[:, WEAVE_SPLIT:, :].rearrange("p (c i) j -> p c j i", i=4),
-            in_=coarse[:, :, WEAVE_SPLIT:].rearrange("p j (c i) -> p c j i", i=4),
+            out=coarse_grouped[:, COARSE_VECTOR_COLUMNS:, :].rearrange("p (c i) j -> p c j i", i=RUN),
+            in_=coarse[:, :, COARSE_VECTOR_COLUMNS:].rearrange("p j (c i) -> p c j i", i=RUN),
         )
-        coarse_q = quantise(coarse_grouped[:], V, "coarse", "coarse_codes")
-        t_rows = []
-        for m in range(N // P):
+        coarse_q = quantise(coarse_grouped[:], V, "coarse")
+        for m in range(ROW_TILES):
             acc = psum.tile([P, V], F32, name=f"t_acc{m}", tag=f"bank{6 + m}")
             project(w2, m, coarse_q, acc[:])
-            t_row = keep.tile([P, V], F32, name=f"t_row{m}")
-            if m == 0:
-                nc.vector.tensor_copy(out=t_row[:], in_=acc[:])
-            else:
-                nc.scalar.copy(out=t_row[:], in_=acc[:])
-            t_rows.append(t_row)
-        row_tiles = N // P
-        stretches = []
-        first = 0
-        for width in STRETCHES:
-            stretches.append((first, width))
-            first = first + width
-        items = []
-        for c in range(len(stretches)):
-            items.extend([(c, m, 1) for m in range(row_tiles)])
-        parents = {}
-        for c, m0, count in items:
-            parents[c, m0] = keep.tile([P, count, stretches[c][1]], F32, name=f"parent{c}_{m0}", tag=f"parent{c}_{m0}", align_bytes=64)
-        for m in range(row_tiles):
-            for c, m0, count in items:
-                if m0 <= m < m0 + count:
-                    nc.vector.tensor_copy(
-                        out=parents[c, m0][:, m - m0, :],
-                        in_=t_rows[m][:].indirect(entries(par_list, *stretches[c])),
-                    )
+            nc.scalar.copy(out=coarse_tile[:, m * V : (m + 1) * V], in_=acc[:])
 
-        picked = [keep.tile([P, HALF, PACK], BF16, name=f"picked{h}", align_bytes=64) for h in range(2)]
-        rounded = {2: keep.tile([P, T], BF16, name="rounded2", tag="rounded")}
+        parent_rows = []
+        for m in range(ROW_TILES):
+            parent_row = keep.tile([P, S], F32, name=f"parents{m}")
+            nc.vector.tensor_copy(out=parent_row[:], in_=coarse_tile[:, m * V : m * V + PARENT_WINDOW].indirect(par_list[:]))
+            parent_rows.append(parent_row)
 
-        def pick_vector(j, h):
-            nc.vector.tensor_copy(out=picked[h][:, :, j], in_=planes[j].indirect(entries(offs_list, h * HALF, HALF)))
+        picked = keep.tile([P, S, PACK], BF16, name="picked", align_bytes=64)
 
-        def pick_scalar(j, h):
-            nc.scalar.activation(out=picked[h][:, :, j], in_=rounded[j][:].indirect(entries(offs_list, h * HALF, HALF)), func=ACT.Copy)
+        def pick_vector(j, first, count):
+            nc.vector.tensor_copy(out=picked[:, first : first + count, j], in_=planes[j].indirect(entries(offs_list, first, count)))
 
-        def round_shared(j, cols, vector_columns):
-            middle_col = cols.start + vector_columns
-            if vector_columns > 0:
-                nc.vector.tensor_copy(out=rounded[j][:, cols.start : middle_col], in_=planes[j][:, cols.start : middle_col])
-            nc.scalar.copy(out=rounded[j][:, middle_col : cols.stop], in_=planes[j][:, middle_col : cols.stop])
+        def pick_scalar(rounded, j, first, count):
+            nc.scalar.activation(out=picked[:, first : first + count, j], in_=rounded[:].indirect(entries(offs_list, first, count)), func=ACT.Copy)
 
-        round_shared(2, slice(0, T), VECTOR_CAST_PLANE2)
-        pick_scalar(2, 0)
-        pick_scalar(2, 1)
+        def round_columns(rounded, j, first, split, last):
+            if split > first:
+                nc.vector.tensor_copy(out=rounded[:, first:split], in_=planes[j][:, first:split])
+            nc.scalar.copy(out=rounded[:, split:last], in_=planes[j][:, split:last])
+
+        rounded2 = keep.tile([P, T], BF16, name="rounded2", tag="rounded")
+        round_columns(rounded2, 2, 0, PLANE2_VECTOR_COLUMNS, T)
+        pick_scalar(rounded2, 2, 0, S)
         for j in (1, 0):
-            for h in range(2):
-                pick_vector(j, h)
-        rounded[3] = keep.tile([P, T], BF16, name="rounded3", tag="rounded")
-        for cols, vector_columns in zip(pieces, VECTOR_CAST_COLUMNS):
-            round_shared(3, cols, vector_columns)
-        pick_vector(3, 0)
-        pick_scalar(3, 1)
+            pick_vector(j, 0, S)
+        rounded3 = keep.tile([P, T], BF16, name="rounded3", tag="rounded")
+        for first, split, last in pieces:
+            round_columns(rounded3, 3, first, split, last)
+        pick_vector(3, 0, HALF)
+        pick_scalar(rounded3, 3, HALF, HALF)
 
-        out_rows = out.rearrange("(m p) s -> p m s", p=P)
-        sums = {}
-
-        def multiply(c):
-            start, width = stretches[c]
-            h, first = divmod(start, HALF)
-            fine_q = quantise(picked[h][:, first : first + width, :], width, f"fine{c}", f"fine{c}_codes")
-            for i, (ci, m0, count) in enumerate(items):
-                if ci == c:
-                    sums[c, m0] = psum.tile([P, count, width], F32, name=f"y_acc{c}_{m0}", tag=f"bank{i % 8}")
-                    for m in range(count):
-                        project(w1, m0 + m, fine_q, sums[c, m0][:, m, :])
-
-        def finish(c):
-            start, width = stretches[c]
-            for ci, m0, count in items:
-                if ci == c:
-                    total = keep.tile([P, count, width], F32, name=f"total{c}_{m0}")
-                    nc.vector.tensor_tensor(out=total[:], in0=sums[c, m0][:], in1=parents[c, m0][:], op=ALU.add)
-                    result = keep.tile([P, count, width], F32, name=f"result{c}_{m0}")
-                    nc.scalar.activation(out=result[:], in_=total[:], func=ACT.Relu)
-                    queue = nc.scalar if (ci, m0, count) == items[-1] else nc.sync
-                    queue.dma_start(out=out_rows[:, m0 : m0 + count, start : start + width], in_=result[:])
-
-        for c in range(len(stretches)):
-            multiply(c)
-        for c in range(len(stretches)):
-            finish(c)
+        fine_q = []
+        for c in range(S // STRETCH):
+            fine_q.append(quantise(picked[:, c * STRETCH : (c + 1) * STRETCH, :], STRETCH, f"fine{c}"))
+        parts = [(c, m) for c in range(S // STRETCH) for m in range(ROW_TILES)]
+        for i, (c, m) in enumerate(parts):
+            acc = psum.tile([P, STRETCH], F32, name=f"y_acc{c}_{m}", tag=f"bank{i}")
+            project(w1, m, fine_q[c], acc[:])
+            total = keep.tile([P, STRETCH], F32, name=f"total{c}_{m}")
+            nc.vector.tensor_tensor(out=total[:], in0=acc[:], in1=parent_rows[m][:, c * STRETCH : (c + 1) * STRETCH], op=ALU.add)
+            result = keep.tile([P, STRETCH], F32, name=f"result{c}_{m}")
+            nc.scalar.activation(out=result[:], in_=total[:], func=ACT.Relu)
+            queue = nc.scalar if i == len(parts) - 1 else nc.sync
+            queue.dma_start(out=out[P * m : P * (m + 1), c * STRETCH : (c + 1) * STRETCH], in_=result[:])

@@ -25,10 +25,10 @@ LIST_ROWS = 16
 QUADRANT = 32
 RUN = 4
 
-LAST_PLANE_PIECES = ((1536, 0), (1600, 1088), (704, 448), (256, 0))
+LAST_PLANE_PIECES = ((1728, 0), (1408, 1408), (704, 448), (256, 0))
 PLANE2_VECTOR_COLUMNS = 1792
-COARSE_VECTOR_COLUMNS = 336
 PARENT_WINDOW = 1408
+STEP = STRETCH // 2
 
 
 def tile_picked_fpn_relu_e_kernel(tc, xT, sT, w1_words, w1_scales, w2_words, w2_scales, offs, par, out):
@@ -97,18 +97,14 @@ def tile_picked_fpn_relu_e_kernel(tc, xT, sT, w1_words, w1_scales, w2_words, w2_
 
         coarse_grouped = keep.tile([P, V, PACK], BF16, name="coarse_grouped", align_bytes=64)
         nc.vector.tensor_copy(
-            out=coarse_grouped[:, :COARSE_VECTOR_COLUMNS, :].rearrange("p (c i) j -> p c j i", i=RUN),
-            in_=coarse[:, :, :COARSE_VECTOR_COLUMNS].rearrange("p j (c i) -> p c j i", i=RUN),
-        )
-        nc.scalar.copy(
-            out=coarse_grouped[:, COARSE_VECTOR_COLUMNS:, :].rearrange("p (c i) j -> p c j i", i=RUN),
-            in_=coarse[:, :, COARSE_VECTOR_COLUMNS:].rearrange("p j (c i) -> p c j i", i=RUN),
+            out=coarse_grouped[:].rearrange("p (c i) j -> p c j i", i=RUN),
+            in_=coarse.rearrange("p j (c i) -> p c j i", i=RUN),
         )
         coarse_q = quantise(coarse_grouped[:], V, "coarse")
         for m in range(ROW_TILES):
             acc = psum.tile([P, V], F32, name=f"t_acc{m}", tag=f"bank{6 + m}")
             project(w2, m, coarse_q, acc[:])
-            nc.scalar.copy(out=coarse_tile[:, m * V : (m + 1) * V], in_=acc[:])
+            nc.vector.tensor_copy(out=coarse_tile[:, m * V : (m + 1) * V], in_=acc[:])
 
         parent_rows = []
         for m in range(ROW_TILES):
@@ -127,7 +123,8 @@ def tile_picked_fpn_relu_e_kernel(tc, xT, sT, w1_words, w1_scales, w2_words, w2_
         def round_columns(rounded, j, first, split, last):
             if split > first:
                 nc.vector.tensor_copy(out=rounded[:, first:split], in_=planes[j][:, first:split])
-            nc.scalar.copy(out=rounded[:, split:last], in_=planes[j][:, split:last])
+            if last > split:
+                nc.scalar.copy(out=rounded[:, split:last], in_=planes[j][:, split:last])
 
         rounded2 = keep.tile([P, T], BF16, name="rounded2", tag="rounded")
         round_columns(rounded2, 2, 0, PLANE2_VECTOR_COLUMNS, T)
@@ -140,16 +137,24 @@ def tile_picked_fpn_relu_e_kernel(tc, xT, sT, w1_words, w1_scales, w2_words, w2_
         pick_vector(3, 0, HALF)
         pick_scalar(rounded3, 3, HALF, HALF)
 
-        fine_q = []
+        quantised = []
         for c in range(S // STRETCH):
-            fine_q.append(quantise(picked[:, c * STRETCH : (c + 1) * STRETCH, :], STRETCH, f"fine{c}"))
+            first = c * STRETCH
+            width = STRETCH // 2 if c == 0 else STRETCH
+            quantised.append(
+                [quantise(picked[:, a : a + width, :], width, f"fine{c}_{a}") for a in range(first, first + STRETCH, width)]
+            )
         parts = [(c, m) for c in range(S // STRETCH) for m in range(ROW_TILES)]
         for i, (c, m) in enumerate(parts):
             acc = psum.tile([P, STRETCH], F32, name=f"y_acc{c}_{m}", tag=f"bank{i}")
-            project(w1, m, fine_q[c], acc[:])
+            width = STRETCH // len(quantised[c])
+            for a, operand in enumerate(quantised[c]):
+                project(w1, m, operand, acc[:, a * width : (a + 1) * width])
             total = keep.tile([P, STRETCH], F32, name=f"total{c}_{m}")
-            nc.vector.tensor_tensor(out=total[:], in0=acc[:], in1=parent_rows[m][:, c * STRETCH : (c + 1) * STRETCH], op=ALU.add)
             result = keep.tile([P, STRETCH], F32, name=f"result{c}_{m}")
-            nc.scalar.activation(out=result[:], in_=total[:], func=ACT.Relu)
+            for a in range(0, STRETCH, STEP):
+                cols = slice(a, a + STEP)
+                nc.vector.tensor_tensor(out=total[:, cols], in0=acc[:, cols], in1=parent_rows[m][:, c * STRETCH + a : c * STRETCH + a + STEP], op=ALU.add)
+                nc.scalar.activation(out=result[:, cols], in_=total[:, cols], func=ACT.Relu)
             queue = nc.scalar if i == len(parts) - 1 else nc.sync
             queue.dma_start(out=out[P * m : P * (m + 1), c * STRETCH : (c + 1) * STRETCH], in_=result[:])

@@ -19,15 +19,14 @@ ALU = mybir.AluOpType
 P = 128
 PACK = 4
 ROW_TILES = N // P
-HALF = S // 2
-STRETCH = 256
 LIST_ROWS = 16
 QUADRANT = 32
 RUN = 4
-
-LAST_PLANE_PIECES = ((1728, 0), (1408, 1408), (704, 448), (256, 0))
-PLANE2_VECTOR_COLUMNS = 1792
 PARENT_WINDOW = 1408
+
+VECTOR_CELLS = (128, 512)
+SCALAR_PIECES = ((0, 128), (640, 128), (768, 256))
+STRETCH = 256
 STEP = STRETCH // 2
 
 
@@ -51,11 +50,14 @@ def tile_picked_fpn_relu_e_kernel(tc, xT, sT, w1_words, w1_scales, w2_words, w2_
                 )
             return word_tile, scale_tile
 
-        def quantise(grouped, width, name):
-            codes = keep.tile([P, width], U32, name=name + "_codes", align_bytes=64)
-            scales = keep.tile([P, width], U8, name=name + "_scales", align_bytes=64)
-            nc.vector.quantize_mx(out=codes[:].bitcast(FP8X4), scales=scales[:], in_=grouped.rearrange("p w j -> p (w j)"))
+        def quantise(grouped, codes, scales):
+            nc.vector.quantize_mx(out=codes.bitcast(FP8X4), scales=scales, in_=grouped.rearrange("p w j -> p (w j)"))
             return codes, scales
+
+        def quantise_anew(grouped, width, name, tag=None):
+            codes = keep.tile([P, width], U32, name=name + "_codes", tag=tag or name + "_codes", align_bytes=64)
+            scales = keep.tile([P, width], U8, name=name + "_scales", align_bytes=64)
+            return quantise(grouped, codes[:], scales[:])
 
         def project(weights, m, operand, acc):
             word_tile, scale_tile = weights
@@ -64,17 +66,17 @@ def tile_picked_fpn_relu_e_kernel(tc, xT, sT, w1_words, w1_scales, w2_words, w2_
                 out=acc,
                 lhsT=word_tile[:, 2 * P * m : 2 * P * (m + 1)].bitcast(FP4X4),
                 lhsT_scale=scale_tile[:, P * m : P * (m + 1)],
-                rhs=codes[:].bitcast(FP8X4),
-                rhs_scale=scales[:],
+                rhs=codes.bitcast(FP8X4),
+                rhs_scale=scales,
                 start=True,
                 stop=True,
             )
 
         x_rows = xT.rearrange("(p j) t -> p j t", j=PACK)
-        plane0 = keep.tile([P, T], F32, name="plane0")
-        planes12 = keep.tile([P, 2, T], F32, name="planes12")
+        planes01 = keep.tile([P, 2, T], F32, name="planes01")
+        plane2 = keep.tile([P, T], F32, name="plane2")
         plane3 = keep.tile([P, T], F32, name="plane3")
-        planes = [plane0[:], planes12[:, 0, :], planes12[:, 1, :], plane3[:]]
+        planes = [planes01[:, 0, :], planes01[:, 1, :], plane2[:], plane3[:]]
 
         coarse_tile = keep.tile([P, (ROW_TILES + PACK) * V], F32, name="coarse_tile")
         coarse = coarse_tile[:, ROW_TILES * V :].rearrange("p (j v) -> p j v", j=PACK)
@@ -82,17 +84,11 @@ def tile_picked_fpn_relu_e_kernel(tc, xT, sT, w1_words, w1_scales, w2_words, w2_
         par_list = keep.tile([P, S // LIST_ROWS], U16, name="par_list")
         nc.sync.dma_start(par_list[:], par)
         w2 = load_weights(w2_words, w2_scales, "w2")
-        nc.sync.dma_start(out=planes12[:], in_=x_rows[:, 1:3, :])
+        nc.sync.dma_start(out=planes01[:], in_=x_rows[:, 0:2, :])
         offs_list = keep.tile([P, S // LIST_ROWS], U16, name="offs_list")
         nc.sync.dma_start(offs_list[:], offs)
-        nc.sync.dma_start(out=planes[0], in_=x_rows[:, 0, :])
-        pieces = []
-        first = 0
-        for width, vector_columns in LAST_PLANE_PIECES:
-            pieces.append((first, first + vector_columns, first + width))
-            first = first + width
-        for first, split, last in pieces:
-            nc.sync.dma_start(out=planes[3][:, first:last], in_=x_rows[:, 3, first:last])
+        for j in (2, 3):
+            nc.sync.dma_start(out=planes[j], in_=x_rows[:, j, :])
         w1 = load_weights(w1_words, w1_scales, "w1")
 
         coarse_grouped = keep.tile([P, V, PACK], BF16, name="coarse_grouped", align_bytes=64)
@@ -100,11 +96,11 @@ def tile_picked_fpn_relu_e_kernel(tc, xT, sT, w1_words, w1_scales, w2_words, w2_
             out=coarse_grouped[:].rearrange("p (c i) j -> p c j i", i=RUN),
             in_=coarse.rearrange("p j (c i) -> p c j i", i=RUN),
         )
-        coarse_q = quantise(coarse_grouped[:], V, "coarse")
+        coarse_q = quantise_anew(coarse_grouped[:], V, "coarse")
         for m in range(ROW_TILES):
             acc = psum.tile([P, V], F32, name=f"t_acc{m}", tag=f"bank{6 + m}")
             project(w2, m, coarse_q, acc[:])
-            nc.vector.tensor_copy(out=coarse_tile[:, m * V : (m + 1) * V], in_=acc[:])
+            nc.scalar.copy(out=coarse_tile[:, m * V : (m + 1) * V], in_=acc[:])
 
         parent_rows = []
         for m in range(ROW_TILES):
@@ -113,48 +109,70 @@ def tile_picked_fpn_relu_e_kernel(tc, xT, sT, w1_words, w1_scales, w2_words, w2_
             parent_rows.append(parent_row)
 
         picked = keep.tile([P, S, PACK], BF16, name="picked", align_bytes=64)
+        dense = [keep.tile([P, 2, count], BF16, name=f"dense{i}", tag=f"dense{i}", align_bytes=64) for i, (first, count) in enumerate(SCALAR_PIECES)]
 
         def pick_vector(j, first, count):
             nc.vector.tensor_copy(out=picked[:, first : first + count, j], in_=planes[j].indirect(entries(offs_list, first, count)))
 
-        def pick_scalar(rounded, j, first, count):
-            nc.scalar.activation(out=picked[:, first : first + count, j], in_=rounded[:].indirect(entries(offs_list, first, count)), func=ACT.Copy)
+        def pick_scalar(j, i):
+            first, count = SCALAR_PIECES[i]
+            nc.scalar.activation(out=dense[i][:, j - 2, :], in_=planes[j].indirect(entries(offs_list, first, count)), func=ACT.Copy)
 
-        def round_columns(rounded, j, first, split, last):
-            if split > first:
-                nc.vector.tensor_copy(out=rounded[:, first:split], in_=planes[j][:, first:split])
-            if last > split:
-                nc.scalar.copy(out=rounded[:, split:last], in_=planes[j][:, split:last])
+        def place_scalar(i):
+            first, count = SCALAR_PIECES[i]
+            nc.scalar.copy(out=picked[:, first : first + count, 2:4], in_=dense[i][:].rearrange("p j c -> p c j"))
 
-        rounded2 = keep.tile([P, T], BF16, name="rounded2", tag="rounded")
-        round_columns(rounded2, 2, 0, PLANE2_VECTOR_COLUMNS, T)
-        pick_scalar(rounded2, 2, 0, S)
-        for j in (1, 0):
+        for j in (0, 1):
             pick_vector(j, 0, S)
-        rounded3 = keep.tile([P, T], BF16, name="rounded3", tag="rounded")
-        for first, split, last in pieces:
-            round_columns(rounded3, 3, first, split, last)
-        pick_vector(3, 0, HALF)
-        pick_scalar(rounded3, 3, HALF, HALF)
+        for i in range(len(SCALAR_PIECES)):
+            pick_scalar(2, i)
+        for j in (2, 3):
+            pick_vector(j, *VECTOR_CELLS)
+        pick_scalar(3, 0)
+        pick_scalar(3, 1)
+        place_scalar(0)
+        pick_scalar(3, 2)
+        place_scalar(1)
+        place_scalar(2)
 
-        quantised = []
-        for c in range(S // STRETCH):
-            first = c * STRETCH
-            width = STRETCH // 2 if c == 0 else STRETCH
-            quantised.append(
-                [quantise(picked[:, a : a + width, :], width, f"fine{c}_{a}") for a in range(first, first + STRETCH, width)]
-            )
-        parts = [(c, m) for c in range(S // STRETCH) for m in range(ROW_TILES)]
-        for i, (c, m) in enumerate(parts):
-            acc = psum.tile([P, STRETCH], F32, name=f"y_acc{c}_{m}", tag=f"bank{i}")
-            width = STRETCH // len(quantised[c])
-            for a, operand in enumerate(quantised[c]):
-                project(w1, m, operand, acc[:, a * width : (a + 1) * width])
-            total = keep.tile([P, STRETCH], F32, name=f"total{c}_{m}")
-            result = keep.tile([P, STRETCH], F32, name=f"result{c}_{m}")
-            for a in range(0, STRETCH, STEP):
-                cols = slice(a, a + STEP)
-                nc.vector.tensor_tensor(out=total[:, cols], in0=acc[:, cols], in1=parent_rows[m][:, c * STRETCH + a : c * STRETCH + a + STEP], op=ALU.add)
-                nc.scalar.activation(out=result[:, cols], in_=total[:, cols], func=ACT.Relu)
-            queue = nc.scalar if i == len(parts) - 1 else nc.sync
+        first_q = quantise_anew(picked[:, 0:STEP, :], STEP, "first")
+        own_codes = keep.tile([P, STEP + STRETCH], U32, name="own_codes", tag="dense0", align_bytes=64)
+        own_scales = keep.tile([P, STEP + STRETCH], U8, name="own_scales", align_bytes=64)
+        second_q = quantise(picked[:, STEP:STRETCH, :], own_codes[:, :STEP], own_scales[:, :STEP])
+        operands = {
+            1: quantise(picked[:, STRETCH : 2 * STRETCH, :], own_codes[:, STEP:], own_scales[:, STEP:]),
+            2: quantise_anew(picked[:, 2 * STRETCH : 3 * STRETCH, :], STRETCH, "third"),
+        }
+
+        def finish(acc, m, first, count, result):
+            total = keep.tile([P, count], F32, name=f"total{m}_{first}")
+            nc.vector.tensor_tensor(out=total[:], in0=acc, in1=parent_rows[m][:, first : first + count], op=ALU.add)
+            nc.scalar.activation(out=result, in_=total[:], func=ACT.Relu)
+
+        def store(c, m, result, queue):
             queue.dma_start(out=out[P * m : P * (m + 1), c * STRETCH : (c + 1) * STRETCH], in_=result[:])
+
+        halves = {}
+        for h, operand in enumerate((first_q, second_q)):
+            for m in range(ROW_TILES):
+                acc = psum.tile([P, STEP], F32, name=f"y_acc0_{h}_{m}", tag=f"bank{2 * h + m}")
+                project(w1, m, operand, acc[:])
+                halves[(h, m)] = acc
+        for m in range(ROW_TILES):
+            result = keep.tile([P, STRETCH], F32, name=f"result0_{m}")
+            for h in range(2):
+                finish(halves[(h, m)][:], m, h * STEP, STEP, result[:, h * STEP : (h + 1) * STEP])
+            store(0, m, result, nc.sync)
+
+        parts = [(c, m) for c in range(1, S // STRETCH) for m in range(ROW_TILES)]
+        for i, (c, m) in enumerate(parts):
+            acc = psum.tile([P, STRETCH], F32, name=f"y_acc{c}_{m}", tag=f"bank{(4 + i) % 8}")
+            project(w1, m, operands[c], acc[:])
+            result = keep.tile([P, STRETCH], F32, name=f"result{c}_{m}")
+            last = i == len(parts) - 1
+            width = STEP if last else STRETCH
+            for a in range(0, STRETCH, width):
+                finish(acc[:, a : a + width], m, c * STRETCH + a, width, result[:, a : a + width])
+            store(c, m, result, nc.scalar if last else nc.sync)
+            if i == 0:
+                operands[3] = quantise_anew(picked[:, 3 * STRETCH :, :], STRETCH, "fourth", tag="dense0")

@@ -25,9 +25,11 @@ RUN = 4
 PARENT_WINDOW = 1408
 
 VECTOR_CELLS = (128, 512)
-SCALAR_PIECES = ((0, 128), (640, 128), (768, 256))
+SCALAR_RUNS = ((0, 128), (640, 384))
+SCALAR_PIECES = ((0, 128), (640, 128), (768, 128), (896, 128))
 STRETCH = 256
 STEP = STRETCH // 2
+HALVED = (1, 2)
 
 
 def tile_picked_fpn_relu_e_kernel(tc, xT, sT, w1_words, w1_scales, w2_words, w2_scales, offs, par, out):
@@ -100,7 +102,8 @@ def tile_picked_fpn_relu_e_kernel(tc, xT, sT, w1_words, w1_scales, w2_words, w2_
         for m in range(ROW_TILES):
             acc = psum.tile([P, V], F32, name=f"t_acc{m}", tag=f"bank{6 + m}")
             project(w2, m, coarse_q, acc[:])
-            nc.scalar.copy(out=coarse_tile[:, m * V : (m + 1) * V], in_=acc[:])
+            copy_out = nc.scalar.copy if m == 0 else nc.vector.tensor_copy
+            copy_out(out=coarse_tile[:, m * V : (m + 1) * V], in_=acc[:])
 
         parent_rows = []
         for m in range(ROW_TILES):
@@ -109,51 +112,63 @@ def tile_picked_fpn_relu_e_kernel(tc, xT, sT, w1_words, w1_scales, w2_words, w2_
             parent_rows.append(parent_row)
 
         picked = keep.tile([P, S, PACK], BF16, name="picked", align_bytes=64)
-        dense = [keep.tile([P, 2, count], BF16, name=f"dense{i}", tag=f"dense{i}", align_bytes=64) for i, (first, count) in enumerate(SCALAR_PIECES)]
 
         def pick_vector(j, first, count):
             nc.vector.tensor_copy(out=picked[:, first : first + count, j], in_=planes[j].indirect(entries(offs_list, first, count)))
 
-        def pick_scalar(j, i):
-            first, count = SCALAR_PIECES[i]
-            nc.scalar.activation(out=dense[i][:, j - 2, :], in_=planes[j].indirect(entries(offs_list, first, count)), func=ACT.Copy)
+        def pick_scalar(j, first, count):
+            dense = keep.tile([P, count], BF16, name=f"dense{j}_{first}", tag=f"dense{j}_{first}", align_bytes=64)
+            nc.scalar.activation(out=dense[:], in_=planes[j].indirect(entries(offs_list, first, count)), func=ACT.Copy)
+            return dense, j, first, count
 
-        def place_scalar(i):
-            first, count = SCALAR_PIECES[i]
-            nc.scalar.copy(out=picked[:, first : first + count, 2:4], in_=dense[i][:].rearrange("p j c -> p c j"))
+        def place_scalar(dense, j, first, count):
+            nc.scalar.copy(out=picked[:, first : first + count, j], in_=dense[:])
 
         for j in (0, 1):
             pick_vector(j, 0, S)
-        for i in range(len(SCALAR_PIECES)):
-            pick_scalar(2, i)
+        for piece in [pick_scalar(2, *run) for run in SCALAR_RUNS]:
+            place_scalar(*piece)
         for j in (2, 3):
             pick_vector(j, *VECTOR_CELLS)
-        pick_scalar(3, 0)
-        pick_scalar(3, 1)
-        place_scalar(0)
-        pick_scalar(3, 2)
-        place_scalar(1)
-        place_scalar(2)
+        behind = None
+        for run in SCALAR_PIECES:
+            piece = pick_scalar(3, *run)
+            if behind:
+                place_scalar(*behind)
+            behind = piece
+        place_scalar(*behind)
 
-        first_q = quantise_anew(picked[:, 0:STEP, :], STEP, "first")
-        own_codes = keep.tile([P, STEP + STRETCH], U32, name="own_codes", tag="dense0", align_bytes=64)
-        own_scales = keep.tile([P, STEP + STRETCH], U8, name="own_scales", align_bytes=64)
-        second_q = quantise(picked[:, STEP:STRETCH, :], own_codes[:, :STEP], own_scales[:, :STEP])
-        operands = {
-            1: quantise(picked[:, STRETCH : 2 * STRETCH, :], own_codes[:, STEP:], own_scales[:, STEP:]),
-            2: quantise_anew(picked[:, 2 * STRETCH : 3 * STRETCH, :], STRETCH, "third"),
-        }
+        def quantise_piece(i, tag):
+            first, count = SCALAR_PIECES[i]
+            return quantise_anew(picked[:, first : first + count, :], count, f"piece{i}", tag=tag)
 
-        def finish(acc, m, first, count, result):
+        own_first, own_count = VECTOR_CELLS
+        own_scales = keep.tile([P, own_count], U8, name="own_scales", tag="dense3_0", align_bytes=64)
+
+        def quantise_own(first, count):
+            codes = keep.tile([P, count], U32, name=f"own_codes{first}", tag=f"own_codes{first}", align_bytes=64)
+            return quantise(picked[:, first : first + count, :], codes[:], own_scales[:, first - own_first : first - own_first + count])
+
+        operands = [
+            [quantise_piece(0, "piece_codes"), quantise_own(STEP, STEP)],
+            [quantise_own(STRETCH, STRETCH)],
+            [quantise_own(2 * STRETCH, STEP)],
+            [],
+        ]
+
+        def add(acc, m, first, count):
             total = keep.tile([P, count], F32, name=f"total{m}_{first}")
             nc.vector.tensor_tensor(out=total[:], in0=acc, in1=parent_rows[m][:, first : first + count], op=ALU.add)
-            nc.scalar.activation(out=result, in_=total[:], func=ACT.Relu)
+            return total
+
+        def finish(acc, m, first, count, result):
+            nc.scalar.activation(out=result, in_=add(acc, m, first, count)[:], func=ACT.Relu)
 
         def store(c, m, result, queue):
             queue.dma_start(out=out[P * m : P * (m + 1), c * STRETCH : (c + 1) * STRETCH], in_=result[:])
 
         halves = {}
-        for h, operand in enumerate((first_q, second_q)):
+        for h, operand in enumerate(operands[0]):
             for m in range(ROW_TILES):
                 acc = psum.tile([P, STEP], F32, name=f"y_acc0_{h}_{m}", tag=f"bank{2 * h + m}")
                 project(w1, m, operand, acc[:])
@@ -163,16 +178,24 @@ def tile_picked_fpn_relu_e_kernel(tc, xT, sT, w1_words, w1_scales, w2_words, w2_
             for h in range(2):
                 finish(halves[(h, m)][:], m, h * STEP, STEP, result[:, h * STEP : (h + 1) * STEP])
             store(0, m, result, nc.sync)
+            operands[2 + m].append(quantise_piece(1 + m, ("piece_codes", f"own_codes{STEP}")[m]))
 
         parts = [(c, m) for c in range(1, S // STRETCH) for m in range(ROW_TILES)]
         for i, (c, m) in enumerate(parts):
             acc = psum.tile([P, STRETCH], F32, name=f"y_acc{c}_{m}", tag=f"bank{(4 + i) % 8}")
-            project(w1, m, operands[c], acc[:])
+            width = STRETCH // len(operands[c])
+            for a, operand in enumerate(operands[c]):
+                project(w1, m, operand, acc[:, a * width : (a + 1) * width])
             result = keep.tile([P, STRETCH], F32, name=f"result{c}_{m}")
-            last = i == len(parts) - 1
-            width = STEP if last else STRETCH
+            if i == len(parts) - 1:
+                totals = [add(acc[:, a : a + STEP], m, c * STRETCH + a, STEP) for a in (0, STEP)]
+                for a, total in zip((0, STEP), totals):
+                    nc.vector.tensor_scalar_max(out=result[:, a : a + STEP], in0=total[:], scalar1=0.0)
+                store(c, m, result, nc.scalar)
+                continue
+            width = STEP if i in HALVED else STRETCH
             for a in range(0, STRETCH, width):
                 finish(acc[:, a : a + width], m, c * STRETCH + a, width, result[:, a : a + width])
-            store(c, m, result, nc.scalar if last else nc.sync)
+            store(c, m, result, nc.sync)
             if i == 0:
-                operands[3] = quantise_anew(picked[:, 3 * STRETCH :, :], STRETCH, "fourth", tag="dense0")
+                operands[3].append(quantise_piece(3, f"own_codes{STRETCH}"))

@@ -75,10 +75,7 @@ def tile_picked_fpn_relu_e_kernel(tc, xT, sT, w1_words, w1_scales, w2_words, w2_
             )
 
         x_rows = xT.rearrange("(p j) t -> p j t", j=PACK)
-        planes01 = keep.tile([P, 2, T], F32, name="planes01")
-        plane2 = keep.tile([P, T], F32, name="plane2")
-        plane3 = keep.tile([P, T], F32, name="plane3")
-        planes = [planes01[:, 0, :], planes01[:, 1, :], plane2[:], plane3[:]]
+        planes = [keep.tile([P, T], F32, name=f"plane{j}")[:] for j in range(PACK)]
 
         coarse_tile = keep.tile([P, (ROW_TILES + PACK) * V], F32, name="coarse_tile")
         coarse = coarse_tile[:, ROW_TILES * V :].rearrange("p (j v) -> p j v", j=PACK)
@@ -86,10 +83,10 @@ def tile_picked_fpn_relu_e_kernel(tc, xT, sT, w1_words, w1_scales, w2_words, w2_
         par_list = keep.tile([P, S // LIST_ROWS], U16, name="par_list")
         nc.sync.dma_start(par_list[:], par)
         w2 = load_weights(w2_words, w2_scales, "w2")
-        nc.sync.dma_start(out=planes01[:], in_=x_rows[:, 0:2, :])
+        nc.sync.dma_start(out=planes[0], in_=x_rows[:, 0, :])
         offs_list = keep.tile([P, S // LIST_ROWS], U16, name="offs_list")
         nc.sync.dma_start(offs_list[:], offs)
-        for j in (2, 3):
+        for j in range(1, PACK):
             nc.sync.dma_start(out=planes[j], in_=x_rows[:, j, :])
         w1 = load_weights(w1_words, w1_scales, "w1")
 

@@ -22,10 +22,9 @@ ROW_TILES = N // P
 LIST_ROWS = 16
 QUADRANT = 32
 RUN = 4
-PARENT_WINDOW = 1408
+PARENT_WINDOW = S + LIST_ROWS
 
 VECTOR_CELLS = (128, 512)
-SCALAR_RUNS = ((0, 128), (640, 384))
 SCALAR_PIECES = ((0, 128), (640, 128), (768, 128), (896, 128))
 STRETCH = 256
 STEP = STRETCH // 2
@@ -75,17 +74,16 @@ def tile_picked_fpn_relu_e_kernel(tc, xT, sT, w1_words, w1_scales, w2_words, w2_
             )
 
         x_rows = xT.rearrange("(p j) t -> p j t", j=PACK)
-        planes = [keep.tile([P, T], F32, name=f"plane{j}")[:] for j in range(PACK)]
+        planes = [keep.tile([P, T], F32, name=f"plane{j}", tag=f"plane{j}", align_bytes=64)[:] for j in range(PACK)]
 
-        coarse_tile = keep.tile([P, (ROW_TILES + PACK) * V], F32, name="coarse_tile")
-        coarse = coarse_tile[:, ROW_TILES * V :].rearrange("p (j v) -> p j v", j=PACK)
-        nc.sync.dma_start(out=coarse, in_=sT.rearrange("(p j) v -> p j v", j=PACK))
+        coarse = keep.tile([P, PACK, V], F32, name="coarse")
+        nc.sync.dma_start(out=coarse[:], in_=sT.rearrange("(p j) v -> p j v", j=PACK))
         par_list = keep.tile([P, S // LIST_ROWS], U16, name="par_list")
         nc.sync.dma_start(par_list[:], par)
-        w2 = load_weights(w2_words, w2_scales, "w2")
         nc.sync.dma_start(out=planes[0], in_=x_rows[:, 0, :])
         offs_list = keep.tile([P, S // LIST_ROWS], U16, name="offs_list")
         nc.sync.dma_start(offs_list[:], offs)
+        w2 = load_weights(w2_words, w2_scales, "w2")
         for j in range(1, PACK):
             nc.sync.dma_start(out=planes[j], in_=x_rows[:, j, :])
         w1 = load_weights(w1_words, w1_scales, "w1")
@@ -93,19 +91,18 @@ def tile_picked_fpn_relu_e_kernel(tc, xT, sT, w1_words, w1_scales, w2_words, w2_
         coarse_grouped = keep.tile([P, V, PACK], BF16, name="coarse_grouped", align_bytes=64)
         nc.vector.tensor_copy(
             out=coarse_grouped[:].rearrange("p (c i) j -> p c j i", i=RUN),
-            in_=coarse.rearrange("p j (c i) -> p c j i", i=RUN),
+            in_=coarse[:].rearrange("p j (c i) -> p c j i", i=RUN),
         )
         coarse_q = quantise_anew(coarse_grouped[:], V, "coarse")
-        for m in range(ROW_TILES):
-            acc = psum.tile([P, V], F32, name=f"t_acc{m}", tag=f"bank{6 + m}")
-            project(w2, m, coarse_q, acc[:])
-            copy_out = nc.scalar.copy if m == 0 else nc.vector.tensor_copy
-            copy_out(out=coarse_tile[:, m * V : (m + 1) * V], in_=acc[:])
-
         parent_rows = []
         for m in range(ROW_TILES):
+            window = keep.tile([P, PARENT_WINDOW], F32, name=f"t_window{m}")
+            nc.vector.memset(window[:, V:], 0.0)
+            acc = psum.tile([P, V], F32, name=f"t_acc{m}", tag=f"bank{6 + m}")
+            project(w2, m, coarse_q, acc[:])
+            nc.vector.tensor_copy(out=window[:, :V], in_=acc[:])
             parent_row = keep.tile([P, S], F32, name=f"parents{m}")
-            nc.vector.tensor_copy(out=parent_row[:], in_=coarse_tile[:, m * V : m * V + PARENT_WINDOW].indirect(par_list[:]))
+            nc.scalar.activation(out=parent_row[:], in_=window[:].indirect(par_list[:]), func=ACT.Copy)
             parent_rows.append(parent_row)
 
         picked = keep.tile([P, S, PACK], BF16, name="picked", align_bytes=64)
@@ -113,34 +110,32 @@ def tile_picked_fpn_relu_e_kernel(tc, xT, sT, w1_words, w1_scales, w2_words, w2_
         def pick_vector(j, first, count):
             nc.vector.tensor_copy(out=picked[:, first : first + count, j], in_=planes[j].indirect(entries(offs_list, first, count)))
 
-        def pick_scalar(j, first, count):
-            dense = keep.tile([P, count], BF16, name=f"dense{j}_{first}", tag=f"dense{j}_{first}", align_bytes=64)
-            nc.scalar.activation(out=dense[:], in_=planes[j].indirect(entries(offs_list, first, count)), func=ACT.Copy)
-            return dense, j, first, count
-
-        def place_scalar(dense, j, first, count):
-            nc.scalar.copy(out=picked[:, first : first + count, j], in_=dense[:])
-
-        for j in (0, 1):
+        for j in range(PACK - 1):
             pick_vector(j, 0, S)
-        for piece in [pick_scalar(2, *run) for run in SCALAR_RUNS]:
-            place_scalar(*piece)
-        for j in (2, 3):
-            pick_vector(j, *VECTOR_CELLS)
-        behind = None
-        for run in SCALAR_PIECES:
-            piece = pick_scalar(3, *run)
-            if behind:
-                place_scalar(*behind)
-            behind = piece
-        place_scalar(*behind)
+        pick_vector(3, *VECTOR_CELLS)
+
+        def pick_scalar(i):
+            first, count = SCALAR_PIECES[i]
+            dense = keep.tile([P, count], BF16, name=f"dense{i}", tag="plane2" if i == 1 else f"dense{i}", align_bytes=64)
+            nc.scalar.activation(out=dense[:], in_=planes[3].indirect(entries(offs_list, first, count)), func=ACT.Copy)
+            return dense
+
+        def place_scalar(i, dense):
+            first, count = SCALAR_PIECES[i]
+            nc.scalar.copy(out=picked[:, first : first + count, 3], in_=dense[:])
+
+        dense_tiles = [pick_scalar(0)]
+        for i in range(1, len(SCALAR_PIECES)):
+            dense_tiles.append(pick_scalar(i))
+            place_scalar(i - 1, dense_tiles[i - 1])
+        place_scalar(len(SCALAR_PIECES) - 1, dense_tiles[-1])
 
         def quantise_piece(i, tag):
             first, count = SCALAR_PIECES[i]
             return quantise_anew(picked[:, first : first + count, :], count, f"piece{i}", tag=tag)
 
         own_first, own_count = VECTOR_CELLS
-        own_scales = keep.tile([P, own_count], U8, name="own_scales", tag="dense3_0", align_bytes=64)
+        own_scales = keep.tile([P, own_count], U8, name="own_scales", tag="dense0", align_bytes=64)
 
         def quantise_own(first, count):
             codes = keep.tile([P, count], U32, name=f"own_codes{first}", tag=f"own_codes{first}", align_bytes=64)

@@ -28,7 +28,7 @@ VECTOR_CELLS = (128, 512)
 SCALAR_PIECES = ((0, 128), (640, 128), (768, 128), (896, 128))
 STRETCH = 256
 STEP = STRETCH // 2
-HALVED = (1, 2)
+HALVED = (1, 2, 3, 4)
 
 
 def tile_picked_fpn_relu_e_kernel(tc, xT, sT, w1_words, w1_scales, w2_words, w2_scales, offs, par, out):
@@ -135,7 +135,7 @@ def tile_picked_fpn_relu_e_kernel(tc, xT, sT, w1_words, w1_scales, w2_words, w2_
             return quantise_anew(picked[:, first : first + count, :], count, f"piece{i}", tag=tag)
 
         own_first, own_count = VECTOR_CELLS
-        own_scales = keep.tile([P, own_count], U8, name="own_scales", tag="dense0", align_bytes=64)
+        own_scales = keep.tile([P, STEP + STRETCH], U8, name="own_scales", tag="dense0", align_bytes=64)
 
         def quantise_own(first, count):
             codes = keep.tile([P, count], U32, name=f"own_codes{first}", tag=f"own_codes{first}", align_bytes=64)
@@ -144,7 +144,7 @@ def tile_picked_fpn_relu_e_kernel(tc, xT, sT, w1_words, w1_scales, w2_words, w2_
         operands = [
             [quantise_piece(0, "piece_codes"), quantise_own(STEP, STEP)],
             [quantise_own(STRETCH, STRETCH)],
-            [quantise_own(2 * STRETCH, STEP)],
+            [quantise_anew(picked[:, 2 * STRETCH : 3 * STRETCH, :], STRETCH, "third")],
             [],
         ]
 
@@ -170,7 +170,7 @@ def tile_picked_fpn_relu_e_kernel(tc, xT, sT, w1_words, w1_scales, w2_words, w2_
             for h in range(2):
                 finish(halves[(h, m)][:], m, h * STEP, STEP, result[:, h * STEP : (h + 1) * STEP])
             store(0, m, result, nc.sync)
-            operands[2 + m].append(quantise_piece(1 + m, ("piece_codes", f"own_codes{STEP}")[m]))
+        operands[3].append(quantise_piece(2, f"own_codes{STEP}"))
 
         parts = [(c, m) for c in range(1, S // STRETCH) for m in range(ROW_TILES)]
         for i, (c, m) in enumerate(parts):

@@ -172,22 +172,33 @@ def tile_picked_fpn_relu_e_kernel(tc, xT, sT, w1_words, w1_scales, w2_words, w2_
             store(0, m, result, nc.sync)
         operands[3].append(quantise_piece(2, f"own_codes{STEP}"))
 
-        parts = [(c, m) for c in range(1, S // STRETCH) for m in range(ROW_TILES)]
+        parts = [(1, 0), (1, 1), (2, 0), (3, 0), (2, 1), (3, 1)]
+        last_result = keep.tile([P, 2 * STRETCH], F32, name="last_result")
         for i, (c, m) in enumerate(parts):
-            acc = psum.tile([P, STRETCH], F32, name=f"y_acc{c}_{m}", tag=f"bank{(4 + i) % 8}")
-            width = STRETCH // len(operands[c])
-            for a, operand in enumerate(operands[c]):
-                project(w1, m, operand, acc[:, a * width : (a + 1) * width])
-            result = keep.tile([P, STRETCH], F32, name=f"result{c}_{m}")
+            if (c, m) == (3, 0):
+                accs = [psum.tile([P, STEP], F32, name=f"y_acc3_0_{a}", tag=f"bank{b}")[:] for a, b in enumerate((7, 2))]
+                for operand, acc in zip(operands[c], accs):
+                    project(w1, m, operand, acc)
+            else:
+                acc = psum.tile([P, STRETCH], F32, name=f"y_acc{c}_{m}", tag=f"bank{(4 + i) % 8}")
+                width = STRETCH // len(operands[c])
+                for a, operand in enumerate(operands[c]):
+                    project(w1, m, operand, acc[:, a * width : (a + 1) * width])
+                accs = [acc[:, :STEP], acc[:, STEP:]] if i in HALVED or i == len(parts) - 1 else [acc[:]]
+            if c >= 2 and m == 1:
+                result = last_result[:, (c - 2) * STRETCH : (c - 1) * STRETCH]
+            else:
+                result = keep.tile([P, STRETCH], F32, name=f"result{c}_{m}")
             if i == len(parts) - 1:
-                totals = [add(acc[:, a : a + STEP], m, c * STRETCH + a, STEP) for a in (0, STEP)]
-                for a, total in zip((0, STEP), totals):
-                    nc.vector.tensor_scalar_max(out=result[:, a : a + STEP], in0=total[:], scalar1=0.0)
-                store(c, m, result, nc.scalar)
+                totals = [add(accs[a], m, c * STRETCH + a * STEP, STEP) for a in range(2)]
+                for a, total in enumerate(totals):
+                    nc.vector.tensor_scalar_max(out=result[:, a * STEP : (a + 1) * STEP], in0=total[:], scalar1=0.0)
+                nc.sync.dma_start(out=out[P:, 2 * STRETCH :], in_=last_result[:])
                 continue
-            width = STEP if i in HALVED else STRETCH
-            for a in range(0, STRETCH, width):
-                finish(acc[:, a : a + width], m, c * STRETCH + a, width, result[:, a : a + width])
-            store(c, m, result, nc.sync)
+            width = STRETCH // len(accs)
+            for a, acc in enumerate(accs):
+                finish(acc, m, c * STRETCH + a * width, width, result[:, a * width : (a + 1) * width])
+            if (c, m) != (2, 1):
+                store(c, m, result, nc.sync)
             if i == 0:
                 operands[3].append(quantise_piece(3, f"own_codes{STRETCH}"))

@@ -28,7 +28,6 @@ VECTOR_CELLS = (128, 512)
 SCALAR_PIECES = ((0, 128), (640, 128), (768, 128), (896, 128))
 STRETCH = 256
 STEP = STRETCH // 2
-HALVED = (1, 2, 3, 4)
 
 
 def tile_picked_fpn_relu_e_kernel(tc, xT, sT, w1_words, w1_scales, w2_words, w2_scales, offs, par, out):
@@ -97,10 +96,10 @@ def tile_picked_fpn_relu_e_kernel(tc, xT, sT, w1_words, w1_scales, w2_words, w2_
         parent_rows = []
         for m in range(ROW_TILES):
             window = keep.tile([P, PARENT_WINDOW], F32, name=f"t_window{m}")
-            nc.vector.memset(window[:, V:], 0.0)
+            nc.gpsimd.memset(window[:, V:], 0.0)
             acc = psum.tile([P, V], F32, name=f"t_acc{m}", tag=f"bank{6 + m}")
             project(w2, m, coarse_q, acc[:])
-            nc.vector.tensor_copy(out=window[:, :V], in_=acc[:])
+            nc.scalar.copy(out=window[:, :V], in_=acc[:])
             parent_row = keep.tile([P, S], F32, name=f"parents{m}")
             nc.scalar.activation(out=parent_row[:], in_=window[:].indirect(par_list[:]), func=ACT.Copy)
             parent_rows.append(parent_row)
@@ -172,33 +171,41 @@ def tile_picked_fpn_relu_e_kernel(tc, xT, sT, w1_words, w1_scales, w2_words, w2_
             store(0, m, result, nc.sync)
         operands[3].append(quantise_piece(2, f"own_codes{STEP}"))
 
-        parts = [(1, 0), (1, 1), (2, 0), (3, 0), (2, 1), (3, 1)]
+        def product(c, m, bank):
+            acc = psum.tile([P, STRETCH], F32, name=f"y_acc{c}_{m}", tag=f"bank{bank}")
+            width = STRETCH // len(operands[c])
+            for a, operand in enumerate(operands[c]):
+                project(w1, m, operand, acc[:, a * width : (a + 1) * width])
+            return acc
+
+        def finish_halves(acc, c, m, result):
+            for a in (0, STEP):
+                finish(acc[:, a : a + STEP], m, c * STRETCH + a, STEP, result[:, a : a + STEP])
+
+        results = {(c, m): keep.tile([P, STRETCH], F32, name=f"result{c}_{m}") for c, m in ((1, 0), (1, 1), (2, 0), (3, 0))}
+        finish(product(1, 0, 4)[:], 0, STRETCH, STRETCH, results[(1, 0)][:])
+        store(1, 0, results[(1, 0)], nc.sync)
+        operands[3].append(quantise_piece(3, f"own_codes{STRETCH}"))
+        finish_halves(product(1, 1, 5), 1, 1, results[(1, 1)])
+        store(1, 1, results[(1, 1)], nc.sync)
+        finish_halves(product(2, 0, 6), 2, 0, results[(2, 0)])
+        store(2, 0, results[(2, 0)], nc.sync)
+
         last_result = keep.tile([P, 2 * STRETCH], F32, name="last_result")
-        for i, (c, m) in enumerate(parts):
-            if (c, m) == (3, 0):
-                accs = [psum.tile([P, STEP], F32, name=f"y_acc3_0_{a}", tag=f"bank{b}")[:] for a, b in enumerate((7, 2))]
-                for operand, acc in zip(operands[c], accs):
-                    project(w1, m, operand, acc)
-            else:
-                acc = psum.tile([P, STRETCH], F32, name=f"y_acc{c}_{m}", tag=f"bank{(4 + i) % 8}")
-                width = STRETCH // len(operands[c])
-                for a, operand in enumerate(operands[c]):
-                    project(w1, m, operand, acc[:, a * width : (a + 1) * width])
-                accs = [acc[:, :STEP], acc[:, STEP:]] if i in HALVED or i == len(parts) - 1 else [acc[:]]
-            if c >= 2 and m == 1:
-                result = last_result[:, (c - 2) * STRETCH : (c - 1) * STRETCH]
-            else:
-                result = keep.tile([P, STRETCH], F32, name=f"result{c}_{m}")
-            if i == len(parts) - 1:
-                totals = [add(accs[a], m, c * STRETCH + a * STEP, STEP) for a in range(2)]
-                for a, total in enumerate(totals):
-                    nc.vector.tensor_scalar_max(out=result[:, a * STEP : (a + 1) * STEP], in0=total[:], scalar1=0.0)
-                nc.sync.dma_start(out=out[P:, 2 * STRETCH :], in_=last_result[:])
-                continue
-            width = STRETCH // len(accs)
-            for a, acc in enumerate(accs):
-                finish(acc, m, c * STRETCH + a * width, width, result[:, a * width : (a + 1) * width])
-            if (c, m) != (2, 1):
-                store(c, m, result, nc.sync)
-            if i == 0:
-                operands[3].append(quantise_piece(3, f"own_codes{STRETCH}"))
+        last_total = keep.tile([P, STRETCH + STEP], F32, name="last_total")
+        piece_accs = [psum.tile([P, STEP], F32, name=f"y_acc3_0_{a}", tag=f"bank{b}") for a, b in enumerate((7, 2))]
+        project(w1, 0, operands[3][0], piece_accs[0][:])
+        finish(piece_accs[0][:], 0, 3 * STRETCH, STEP, results[(3, 0)][:, :STEP])
+        third = product(2, 1, 0)
+        project(w1, 0, operands[3][1], piece_accs[1][:])
+        early = add(third[:, :STEP], 1, 2 * STRETCH, STEP)
+        finish(piece_accs[1][:], 0, 3 * STRETCH + STEP, STEP, results[(3, 0)][:, STEP:])
+        nc.scalar.activation(out=last_result[:, :STEP], in_=early[:], func=ACT.Relu)
+        store(3, 0, results[(3, 0)], nc.sync)
+        fourth = product(3, 1, 1)
+        for a, acc in enumerate((third[:, STEP:], fourth[:, :STEP], fourth[:, STEP:])):
+            first = 2 * STRETCH + (a + 1) * STEP
+            nc.vector.tensor_tensor(out=last_total[:, a * STEP : (a + 1) * STEP], in0=acc, in1=parent_rows[1][:, first : first + STEP], op=ALU.add)
+        for first, end in ((0, STRETCH), (STRETCH, STRETCH + STEP)):
+            nc.vector.tensor_scalar_max(out=last_result[:, STEP + first : STEP + end], in0=last_total[:, first:end], scalar1=0.0)
+        nc.sync.dma_start(out=out[P:, 2 * STRETCH :], in_=last_result[:])

@@ -22,7 +22,6 @@ ROW_TILES = N // P
 LIST_ROWS = 16
 QUADRANT = 32
 RUN = 4
-PARENT_WINDOW = S + LIST_ROWS
 
 VECTOR_CELLS = (128, 512)
 SCALAR_PIECES = ((0, 128), (640, 128), (768, 128), (896, 128))
@@ -75,8 +74,9 @@ def tile_picked_fpn_relu_e_kernel(tc, xT, sT, w1_words, w1_scales, w2_words, w2_
         x_rows = xT.rearrange("(p j) t -> p j t", j=PACK)
         planes = [keep.tile([P, T], F32, name=f"plane{j}", tag=f"plane{j}", align_bytes=64)[:] for j in range(PACK)]
 
-        coarse = keep.tile([P, PACK, V], F32, name="coarse")
-        nc.sync.dma_start(out=coarse[:], in_=sT.rearrange("(p j) v -> p j v", j=PACK))
+        windows = [keep.tile([P, V + spare], F32, name=f"t_window{m}") for m, spare in enumerate((PACK * V, S))]
+        coarse = windows[0][:, V:]
+        nc.sync.dma_start(out=coarse, in_=sT.rearrange("(p j) v -> p (j v)", j=PACK))
         par_list = keep.tile([P, S // LIST_ROWS], U16, name="par_list")
         nc.sync.dma_start(par_list[:], par)
         nc.sync.dma_start(out=planes[0], in_=x_rows[:, 0, :])
@@ -90,19 +90,15 @@ def tile_picked_fpn_relu_e_kernel(tc, xT, sT, w1_words, w1_scales, w2_words, w2_
         coarse_grouped = keep.tile([P, V, PACK], BF16, name="coarse_grouped", align_bytes=64)
         nc.vector.tensor_copy(
             out=coarse_grouped[:].rearrange("p (c i) j -> p c j i", i=RUN),
-            in_=coarse[:].rearrange("p j (c i) -> p c j i", i=RUN),
+            in_=coarse.rearrange("p (j c i) -> p c j i", j=PACK, i=RUN),
         )
         coarse_q = quantise_anew(coarse_grouped[:], V, "coarse")
-        parent_rows = []
+        parent_rows = [windows[1][:, V:], keep.tile([P, S], F32, name="parents1")[:]]
         for m in range(ROW_TILES):
-            window = keep.tile([P, PARENT_WINDOW], F32, name=f"t_window{m}")
-            nc.gpsimd.memset(window[:, V:], 0.0)
             acc = psum.tile([P, V], F32, name=f"t_acc{m}", tag=f"bank{6 + m}")
             project(w2, m, coarse_q, acc[:])
-            nc.scalar.copy(out=window[:, :V], in_=acc[:])
-            parent_row = keep.tile([P, S], F32, name=f"parents{m}")
-            nc.scalar.activation(out=parent_row[:], in_=window[:].indirect(par_list[:]), func=ACT.Copy)
-            parent_rows.append(parent_row)
+            nc.scalar.copy(out=windows[m][:, :V], in_=acc[:])
+            nc.scalar.activation(out=parent_rows[m], in_=windows[m][:].indirect(par_list[:]), func=ACT.Copy)
 
         picked = keep.tile([P, S, PACK], BF16, name="picked", align_bytes=64)
 

from contextlib import ExitStack

import concourse.mybir as mybir

K, T, S, V, N = 512, 4096, 1024, 512, 256
FLOPS = 2 * K * N * (S + V)

F32 = mybir.dt.float32
BF16 = mybir.dt.bfloat16
I32 = mybir.dt.int32
U32 = mybir.dt.uint32
U16 = mybir.dt.uint16
U8 = mybir.dt.uint8
FP8X4 = mybir.dt.float8_e4m3fn_x4
FP4X4 = mybir.dt.float4_e2m1fn_x4
ACT = mybir.ActivationFunctionType
ALU = mybir.AluOpType

P = 128
PACK = 4
ROW_TILES = N // P
LIST_ROWS = 16
QUADRANT = 32
RUN = 4

VECTOR_CELLS = (128, 512)
SCALAR_PIECES = ((0, 128), (640, 128), (768, 128), (896, 128))
STRETCH = 256
STEP = STRETCH // 2


def tile_picked_fpn_relu_e_kernel(tc, xT, sT, w1_words, w1_scales, w2_words, w2_scales, offs, par, out):
    nc = tc.nc
    with ExitStack() as ctx:
        keep = ctx.enter_context(tc.tile_pool(name="keep", bufs=1))
        psum = ctx.enter_context(tc.psum_pool(name="psum", bufs=1))

        def entries(list_tile, start, count):
            return list_tile[:, start // LIST_ROWS : (start + count) // LIST_ROWS]

        def load_weights(words, scales, name):
            word_tile = keep.tile([P, 2 * N], U8, name=name + "_words", align_bytes=64)
            scale_tile = keep.tile([P, N], U8, name=name + "_scales", align_bytes=64)
            nc.sync.dma_start(out=word_tile[:].bitcast(I32), in_=words[0].bitcast(I32))
            for q in range(P // QUADRANT):
                nc.sync.dma_start(
                    out=scale_tile[QUADRANT * q : QUADRANT * q + 4, :].bitcast(I32),
                    in_=scales[0, 4 * q : 4 * q + 4, :].bitcast(I32),
                )
            return word_tile, scale_tile

        def quantise(grouped, codes, scales):
            nc.vector.quantize_mx(out=codes.bitcast(FP8X4), scales=scales, in_=grouped.rearrange("p w j -> p (w j)"))
            return codes, scales

        def quantise_anew(grouped, width, name, tag=None):
            codes = keep.tile([P, width], U32, name=name + "_codes", tag=tag or name + "_codes", align_bytes=64)
            scales = keep.tile([P, width], U8, name=name + "_scales", align_bytes=64)
            return quantise(grouped, codes[:], scales[:])

        def project(weights, m, operand, acc):
            word_tile, scale_tile = weights
            codes, scales = operand
            nc.tensor.matmul_mx(
                out=acc,
                lhsT=word_tile[:, 2 * P * m : 2 * P * (m + 1)].bitcast(FP4X4),
                lhsT_scale=scale_tile[:, P * m : P * (m + 1)],
                rhs=codes.bitcast(FP8X4),
                rhs_scale=scales,
                start=True,
                stop=True,
            )

        x_rows = xT.rearrange("(p j) t -> p j t", j=PACK)
        planes = [keep.tile([P, T], F32, name=f"plane{j}", tag=f"plane{j}", align_bytes=64)[:] for j in range(PACK)]

        windows = [keep.tile([P, V + spare], F32, name=f"t_window{m}") for m, spare in enumerate((PACK * V, S))]
        coarse = windows[0][:, V:]
        nc.sync.dma_start(out=coarse, in_=sT.rearrange("(p j) v -> p (j v)", j=PACK))
        par_list = keep.tile([P, S // LIST_ROWS], U16, name="par_list")
        nc.sync.dma_start(par_list[:], par)
        nc.sync.dma_start(out=planes[0], in_=x_rows[:, 0, :])
        offs_list = keep.tile([P, S // LIST_ROWS], U16, name="offs_list")
        nc.sync.dma_start(offs_list[:], offs)
        w2 = load_weights(w2_words, w2_scales, "w2")
        for j in range(1, PACK):
            nc.sync.dma_start(out=planes[j], in_=x_rows[:, j, :])
        w1 = load_weights(w1_words, w1_scales, "w1")

        coarse_grouped = keep.tile([P, V, PACK], BF16, name="coarse_grouped", align_bytes=64)
        nc.vector.tensor_copy(
            out=coarse_grouped[:].rearrange("p (c i) j -> p c j i", i=RUN),
            in_=coarse.rearrange("p (j c i) -> p c j i", j=PACK, i=RUN),
        )
        coarse_q = quantise_anew(coarse_grouped[:], V, "coarse")
        parent_rows = [windows[1][:, V:], keep.tile([P, S], F32, name="parents1")[:]]
        for m in range(ROW_TILES):
            acc = psum.tile([P, V], F32, name=f"t_acc{m}", tag=f"bank{6 + m}")
            project(w2, m, coarse_q, acc[:])
            nc.scalar.copy(out=windows[m][:, :V], in_=acc[:])
            nc.scalar.activation(out=parent_rows[m], in_=windows[m][:].indirect(par_list[:]), func=ACT.Copy)

        picked = keep.tile([P, S, PACK], BF16, name="picked", align_bytes=64)

        def pick_vector(j, first, count):
            nc.vector.tensor_copy(out=picked[:, first : first + count, j], in_=planes[j].indirect(entries(offs_list, first, count)))

        for j in range(PACK - 1):
            pick_vector(j, 0, S)
        pick_vector(3, *VECTOR_CELLS)

        def pick_scalar(i):
            first, count = SCALAR_PIECES[i]
            dense = keep.tile([P, count], BF16, name=f"dense{i}", tag="plane2" if i == 1 else f"dense{i}", align_bytes=64)
            nc.scalar.activation(out=dense[:], in_=planes[3].indirect(entries(offs_list, first, count)), func=ACT.Copy)
            return dense

        def place_scalar(i, dense):
            first, count = SCALAR_PIECES[i]
            nc.scalar.copy(out=picked[:, first : first + count, 3], in_=dense[:])

        dense_tiles = [pick_scalar(0)]
        for i in range(1, len(SCALAR_PIECES)):
            dense_tiles.append(pick_scalar(i))
            place_scalar(i - 1, dense_tiles[i - 1])
        place_scalar(len(SCALAR_PIECES) - 1, dense_tiles[-1])

        def quantise_piece(i, tag):
            first, count = SCALAR_PIECES[i]
            return quantise_anew(picked[:, first : first + count, :], count, f"piece{i}", tag=tag)

        own_first, own_count = VECTOR_CELLS
        own_scales = keep.tile([P, STEP + STRETCH], U8, name="own_scales", tag="dense0", align_bytes=64)

        def quantise_own(first, count):
            codes = keep.tile([P, count], U32, name=f"own_codes{first}", tag=f"own_codes{first}", align_bytes=64)
            return quantise(picked[:, first : first + count, :], codes[:], own_scales[:, first - own_first : first - own_first + count])

        operands = [
            [quantise_piece(0, "piece_codes"), quantise_own(STEP, STEP)],
            [quantise_own(STRETCH, STRETCH)],
            [quantise_anew(picked[:, 2 * STRETCH : 3 * STRETCH, :], STRETCH, "third")],
            [],
        ]

        def add(acc, m, first, count):
            total = keep.tile([P, count], F32, name=f"total{m}_{first}")
            nc.vector.tensor_tensor(out=total[:], in0=acc, in1=parent_rows[m][:, first : first + count], op=ALU.add)
            return total

        def finish(acc, m, first, count, result):
            nc.scalar.activation(out=result, in_=add(acc, m, first, count)[:], func=ACT.Relu)

        def store(c, m, result, queue):
            queue.dma_start(out=out[P * m : P * (m + 1), c * STRETCH : (c + 1) * STRETCH], in_=result[:])

        halves = {}
        for h, operand in enumerate(operands[0]):
            for m in range(ROW_TILES):
                acc = psum.tile([P, STEP], F32, name=f"y_acc0_{h}_{m}", tag=f"bank{2 * h + m}")
                project(w1, m, operand, acc[:])
                halves[(h, m)] = acc
        for m in range(ROW_TILES):
            result = keep.tile([P, STRETCH], F32, name=f"result0_{m}")
            for h in range(2):
                finish(halves[(h, m)][:], m, h * STEP, STEP, result[:, h * STEP : (h + 1) * STEP])
            store(0, m, result, nc.sync)
        operands[3].append(quantise_piece(2, f"own_codes{STEP}"))

        def product(c, m, bank):
            acc = psum.tile([P, STRETCH], F32, name=f"y_acc{c}_{m}", tag=f"bank{bank}")
            width = STRETCH // len(operands[c])
            for a, operand in enumerate(operands[c]):
                project(w1, m, operand, acc[:, a * width : (a + 1) * width])
            return acc

        def finish_halves(acc, c, m, result):
            for a in (0, STEP):
                finish(acc[:, a : a + STEP], m, c * STRETCH + a, STEP, result[:, a : a + STEP])

        results = {(c, m): keep.tile([P, STRETCH], F32, name=f"result{c}_{m}") for c, m in ((1, 0), (1, 1), (2, 0), (3, 0))}
        finish(product(1, 0, 4)[:], 0, STRETCH, STRETCH, results[(1, 0)][:])
        store(1, 0, results[(1, 0)], nc.sync)
        operands[3].append(quantise_piece(3, f"own_codes{STRETCH}"))
        finish_halves(product(1, 1, 5), 1, 1, results[(1, 1)])
        store(1, 1, results[(1, 1)], nc.sync)
        finish_halves(product(2, 0, 6), 2, 0, results[(2, 0)])
        store(2, 0, results[(2, 0)], nc.sync)

        last_result = keep.tile([P, 2 * STRETCH], F32, name="last_result")
        last_total = keep.tile([P, STRETCH + STEP], F32, name="last_total")
        piece_accs = [psum.tile([P, STEP], F32, name=f"y_acc3_0_{a}", tag=f"bank{b}") for a, b in enumerate((7, 2))]
        project(w1, 0, operands[3][0], piece_accs[0][:])
        finish(piece_accs[0][:], 0, 3 * STRETCH, STEP, results[(3, 0)][:, :STEP])
        third = product(2, 1, 0)
        project(w1, 0, operands[3][1], piece_accs[1][:])
        early = add(third[:, :STEP], 1, 2 * STRETCH, STEP)
        finish(piece_accs[1][:], 0, 3 * STRETCH + STEP, STEP, results[(3, 0)][:, STEP:])
        nc.scalar.activation(out=last_result[:, :STEP], in_=early[:], func=ACT.Relu)
        store(3, 0, results[(3, 0)], nc.sync)
        fourth = product(3, 1, 1)
        for a, acc in enumerate((third[:, STEP:], fourth[:, :STEP], fourth[:, STEP:])):
            first = 2 * STRETCH + (a + 1) * STEP
            nc.vector.tensor_tensor(out=last_total[:, a * STEP : (a + 1) * STEP], in0=acc, in1=parent_rows[1][:, first : first + STEP], op=ALU.add)
        for first, end in ((0, STRETCH), (STRETCH, STRETCH + STEP)):
            nc.vector.tensor_scalar_max(out=last_result[:, STEP + first : STEP + end], in0=last_total[:, first:end], scalar1=0.0)
        nc.sync.dma_start(out=out[P:, 2 * STRETCH :], in_=last_result[:])
